import numpy as np
import ml_dtypes


def mxq(x, axis, fmt="e4m3"):
    dtype, down = {"e4m3": (ml_dtypes.float8_e4m3fn, 7), "e5m2": (ml_dtypes.float8_e5m2, 14)}[fmt]
    v = np.moveaxis(np.asarray(x, np.float32).astype(ml_dtypes.bfloat16).astype(np.float64), axis, -1)
    blocks = v.reshape(v.shape[:-1] + (-1, 32))
    amax = np.abs(blocks).max(-1, keepdims=True)
    byte = np.maximum(np.where(amax > 0, np.frexp(amax)[1] - 1 + 127, 0) - down, 1)
    scale = np.exp2(byte - 127.0)
    codes = (blocks / scale).astype(np.float32).astype(dtype).astype(np.float64)
    return np.moveaxis((codes * scale).reshape(v.shape), -1, axis)


WIDE = False


def mx_kscale(k):
    if not WIDE:
        return np.ones(k)
    levels = np.array([10, -10, 5, -5, 0])
    if k % 512:
        return np.exp2(np.random.permutation(np.resize(levels, k // 32))).repeat(32)
    a = np.empty((k // 512, 16))
    for p in range(k // 512):
        a[p, :8] = np.random.permutation(np.resize(levels, 8))
        for g in range(8):
            far = levels[np.abs(levels - a[p, g]) >= 10]
            a[p, g + 8] = far[np.random.randint(len(far))]
    return np.exp2(a.ravel()).repeat(32)


def f64(x):
    return np.asarray(x).astype(np.float64)


def striped(idx):
    return np.tile(idx.reshape(-1, 16).T, (8, 1)).astype(np.uint16)


def unstriped(offs):
    return offs[:16].T.reshape(-1).astype(np.int64)


E2M1 = np.array([0.0, 0.5, 1.0, 1.5, 2.0, 3.0, 4.0, 6.0, -0.0, -0.5, -1.0, -1.5, -2.0, -3.0, -4.0, -6.0])


def pack_weight(w, fmt):
    k, n = w.shape
    w = f64(np.asarray(w, np.float32).astype(ml_dtypes.bfloat16)).reshape(k // 32, 32, n)
    amax = np.abs(w).max(1)
    if fmt == "e4m3":
        byte = np.frexp(amax)[1] - 1 + 127 - 7
    else:
        mant, ex = np.frexp(amax / 6.0)
        byte = np.where(mant > 0.5, ex, ex - 1) + 127
    byte = np.clip(np.where(amax > 0, byte, 1), 1, 254)
    scaled = (w * np.exp2(127.0 - byte)[:, None, :]).reshape(k, n).astype(np.float32)
    by_word = np.ascontiguousarray(scaled.reshape(k // 512, 128, 4, n).transpose(0, 1, 3, 2))
    if fmt == "e4m3":
        words = by_word.astype(ml_dtypes.float8_e4m3fn).view(np.uint8)
    else:
        c = by_word.astype(ml_dtypes.float4_e2m1fn).view(np.uint8) & 0xF
        words = (c[..., 0::2] | (c[..., 1::2] << 4)).reshape(k // 512, 128, 2 * n)
    return np.ascontiguousarray(words), np.ascontiguousarray(byte.astype(np.uint8).reshape(k // 512, 16, n))


def unpack_weight(words, scales, fmt):
    g, _, n = scales.shape
    words = np.ascontiguousarray(words).reshape(g, 128, n, -1)
    if fmt == "e4m3":
        vals = words.view(ml_dtypes.float8_e4m3fn).astype(np.float64)
    else:
        nib = np.empty((g, 128, n, 4), np.uint8)
        nib[..., 0::2] = words & 0xF
        nib[..., 1::2] = words >> 4
        vals = E2M1[nib]
    vals = vals * np.repeat(np.exp2(scales.astype(np.float64) - 127.0), 8, axis=1)[..., None]
    return vals.transpose(0, 1, 3, 2).reshape(g * 512, n)


def relu(v):
    return np.maximum(v, 0.0)


K, T, E, C, N = 512, 768, 24, 128, 128
TOP = 4


def by_expert(wq, xq):
    return np.concatenate([wq[e].T @ xq[:, e * C:(e + 1) * C] for e in range(E)], axis=1)


def setup_inputs():
    n = np.random.standard_normal
    s = mx_kscale(K)[:, None]
    deal = np.repeat(np.arange(E), C).reshape(TOP, T)[:, np.random.permutation(T)]
    deal = np.take_along_axis(deal, np.argsort(np.random.rand(TOP, T), axis=0), axis=0)
    for _ in range(8):
        s_, t_ = np.random.permutation(T).reshape(2, -1); r = np.random.randint(TOP, size=T // 2); x, y = deal[r, s_].copy(), deal[r, t_].copy()
        ok = ~((deal[:, s_] == y).any(0) | (deal[:, t_] == x).any(0)); deal[r[ok], s_[ok]] = y[ok]; deal[r[ok], t_[ok]] = x[ok]
    order = np.lexsort((np.random.rand(TOP * T), deal.reshape(-1)))
    slot_token = order % T; pos = np.empty(TOP * T, np.int64); pos[order] = np.arange(TOP * T); pos = pos.reshape(TOP, T)
    g = np.random.uniform(0.5, 1.5, (TOP, T)); g = g / g.sum(0)
    w = [pack_weight(m, "e2m1") for m in n((E, K, N)) / np.sqrt(K) / s[None]]
    return {
        "xT": (n((K, T)) * s).astype(np.float32),
        "w_words": np.stack([m[0] for m in w]),
        "w_scales": np.stack([m[1] for m in w]),
        "b": (0.3 * n((N, E))).astype(np.float32),
        "gate": np.stack([np.tile(r, (N, 1)) for r in g]).astype(np.float32),
        "offs": striped(slot_token),
        "pos1": striped(pos[0]),
        "pos2": striped(pos[1]),
        "pos3": striped(pos[2]),
        "pos4": striped(pos[3]),
    }


def reference(xT, w_words, w_scales, b, gate, offs, pos1, pos2, pos3, pos4):
    idx = unstriped(offs)
    w = np.stack([unpack_weight(w_words[e], w_scales[e], "e2m1") for e in range(E)])
    xq = mxq(f64(xT)[:, idx], 0, "e4m3")
    y = by_expert(w, xq)
    y = relu(y + np.repeat(f64(b), C, axis=1))
    return sum(f64(gate[r]) * y[:, unstriped(p)] for r, p in enumerate((pos1, pos2, pos3, pos4)))

@@ -1,0 +1,208 @@
+from contextlib import ExitStack
+
+import concourse.mybir as mybir
+from concourse.masks import make_identity
+
+K, T, E, C, N, TOP = 512, 768, 24, 128, 128, 4
+P = 128
+PACK = 4
+S = E * C
+FLOPS = 2 * K * N * S
+
+F32 = mybir.dt.float32
+BF16 = mybir.dt.bfloat16
+U32 = mybir.dt.uint32
+I32 = mybir.dt.int32
+U16 = mybir.dt.uint16
+U8 = mybir.dt.uint8
+FP8X4 = mybir.dt.float8_e4m3fn_x4
+FP4X4 = mybir.dt.float4_e2m1fn_x4
+ADD, MULT, MAX = mybir.AluOpType.add, mybir.AluOpType.mult, mybir.AluOpType.max
+RELU = mybir.ActivationFunctionType.Relu
+
+X_CUTS = (0, 256, 512, 640, 768)
+WINDOW = 2048
+GROUP = 8
+W_LOAD = 8
+
+
+def tile_moe_tk_lin_relu_kernel(
+    tc, xT, w_words, w_scales, b, gate, offs, pos1, pos2, pos3, pos4, out
+):
+    nc = tc.nc
+    with ExitStack() as ctx:
+        keep = ctx.enter_context(tc.tile_pool(name="keep", bufs=1))
+        psum = ctx.enter_context(tc.psum_pool(name="psum", bufs=1))
+
+        x_bytes = keep.tile([P, WINDOW], U8, align_bytes=64, name="x_bytes")
+        nc.gpsimd.memset(x_bytes[:, 0:T], 0)
+        w_planes = keep.tile([P, E, N], U8, align_bytes=64, name="w_planes")
+        nc.vector.memset(w_planes[:].rearrange("p e n -> p (e n)").bitcast(I32), 0)
+        warm = keep.tile([P, 8], F32, name="warm")
+        nc.vector.memset(warm[:], 0.0)
+        warm_out = keep.tile([P, 8], F32, name="warm_out")
+        nc.scalar.activation(warm_out[:], warm[:], RELU)
+
+        ident = keep.tile([P, P], F32, name="ident")
+        make_identity(nc, ident[:])
+
+        x_view = xT.rearrange("(p j) w -> p j w", j=PACK)
+        raws = []
+        for t0, t1 in zip(X_CUTS[:-1], X_CUTS[1:]):
+            raw = keep.tile([P, PACK, t1 - t0], F32, name="raw%d" % t0)
+            nc.sync.dma_start(out=raw[:], in_=x_view[:, :, t0:t1])
+            raws.append(raw)
+        offs_t = keep.tile([P, S // 16], U16, name="offs_t")
+        nc.sync.dma_start(offs_t[:], offs)
+        for q in range(4):
+            nc.sync.dma_start(
+                out=w_planes[32 * q : 32 * q + 4, :, :].bitcast(I32),
+                in_=w_scales[:, 0, 4 * q : 4 * q + 4, :].rearrange("e q n -> q e n").bitcast(I32),
+            )
+        bias = keep.tile([P, E], F32, name="bias")
+        nc.sync.dma_start(out=bias[:], in_=b)
+        ws = []
+        for e0 in range(0, E, W_LOAD):
+            w = keep.tile([P, W_LOAD, 2 * N], U8, align_bytes=64, name="w%d" % e0)
+            nc.sync.dma_start(
+                out=w[:].bitcast(I32),
+                in_=w_words[e0 : e0 + W_LOAD, 0, :, :].rearrange("e p c -> p e c").bitcast(I32),
+            )
+            ws.append(w)
+        pos_ts, gates = [], []
+        for r, pos in enumerate((pos1, pos2, pos3, pos4)):
+            pos_t = keep.tile([P, T // 16], U16, name="pos_t%d" % r)
+            nc.sync.dma_start(pos_t[:], pos)
+            pos_ts.append(pos_t)
+        for r in range(TOP):
+            g = keep.tile([P, T], F32, name="gate%d" % r)
+            nc.sync.dma_start(out=g[:], in_=gate[r])
+            gates.append(g)
+
+        x_words = keep.tile([P, WINDOW], U32, align_bytes=64, name="x_words")
+
+        def interleave(i, grouped, o):
+            width = X_CUTS[i + 1] - X_CUTS[i]
+            share = width * 5 // 8
+            source = raws[i][:].rearrange("p j w -> p w j")
+            nc.scalar.copy(out=grouped[:, o + share : o + width, :], in_=source[:, share:width, :])
+            nc.vector.tensor_copy(out=grouped[:, o : o + share, :], in_=source[:, 0:share, :])
+
+        for q, parts in enumerate(((0,), (1,), (2, 3))):
+            grouped = keep.tile([P, 256, PACK], BF16, align_bytes=64, name="grouped%d" % q)
+            for i in parts:
+                interleave(i, grouped, X_CUTS[i] - 256 * q)
+            nc.vector.quantize_mx(
+                out=x_words[:, 256 * q : 256 * (q + 1)].bitcast(FP8X4),
+                scales=x_bytes[:, 256 * q : 256 * (q + 1)],
+                in_=grouped[:].rearrange("p w j -> p (w j)"),
+            )
+
+        y = keep.tile([P, S], F32, name="y")
+
+        def expert(e, words, planes, col, acc, acc_col):
+            w = ws[e // W_LOAD]
+            nc.tensor.matmul_mx(
+                out=acc[:, acc_col : acc_col + C],
+                lhsT=w[:, e % W_LOAD, :].bitcast(FP4X4),
+                lhsT_scale=w_planes[:, e, :],
+                rhs=words[:, col : col + C].bitcast(FP8X4),
+                rhs_scale=planes[:, col : col + C],
+                start=True,
+                stop=True,
+            )
+
+        def relu_scalar(e, acc, acc_col):
+            nc.scalar.activation(
+                y[:, e * C : (e + 1) * C], acc[:, acc_col : acc_col + C], RELU, bias=bias[:, e : e + 1]
+            )
+
+        def relu_vector(e, acc, acc_col):
+            nc.vector.tensor_scalar(
+                y[:, e * C : (e + 1) * C], acc[:, acc_col : acc_col + C], bias[:, e : e + 1], 0.0, op0=ADD, op1=MAX
+            )
+
+        def gather_words(e0, n):
+            words = keep.tile([P, n * C], U32, align_bytes=64, name="words%d" % e0)
+            nc.vector.tensor_copy(words[:], x_words[:].indirect(offs_t[:, e0 * C // 16 : (e0 + n) * C // 16]))
+            return words
+
+        def gather_planes(e0, n):
+            planes = keep.tile([P, n * C], U8, align_bytes=64, name="planes%d" % e0)
+            window = x_bytes[:, 0:1024] if n == 1 else x_bytes[:]
+            nc.vector.tensor_copy(planes[:], window.indirect(offs_t[:, e0 * C // 16 : (e0 + n) * C // 16]))
+            return planes
+
+        banks_used = []
+
+        def experts(e0, n, words, planes):
+            acc = psum.tile([P, 512], F32, name="bank%d" % (len(banks_used) % 8))
+            banks_used.append(e0)
+            for i in range(n):
+                expert(e0 + i, words[:, i * C :], planes[:, i * C :], 0, acc, i * C)
+            return acc
+
+        for e0 in range(0, E, GROUP):
+            words = gather_words(e0, GROUP)
+            first = e0
+            for n in (8,) if e0 + GROUP < E else (4, 2, 1, 1):
+                planes = gather_planes(first, n)
+                m = min(4, n)
+                for h in range(0, n, m):
+                    acc = experts(first + h, m, words[:, (first + h - e0) * C :], planes[:, h * C :])
+                    for i in range(m):
+                        if first + h + i < E - 2:
+                            relu_scalar(first + h + i, acc, i * C)
+                        else:
+                            relu_vector(first + h + i, acc, i * C)
+                first += n
+
+        prods = []
+        for r in range(TOP):
+            prod = keep.tile([P, T], F32, name="prod%d" % r)
+            prods.append(prod)
+
+        def fetch(r, lo, hi):
+            nc.vector.tensor_tensor(
+                prods[r][:, lo:hi], y[:].indirect(pos_ts[r][:, lo // 16 : hi // 16]), gates[r][:, lo:hi], MULT
+            )
+
+        blocks = T // P
+        sums_t = []
+        for k in range(blocks):
+            sum_t = psum.tile([P, 512], F32, name="bank%d" % k)
+            sums_t.append(sum_t)
+        back_a = psum.tile([P, 512], F32, name="bank6")
+        back_b = psum.tile([P, 512], F32, name="bank7")
+
+        def add_turned(r, k):
+            nc.tensor.matmul(
+                out=sums_t[k][:, 0:P],
+                lhsT=prods[r][:, k * P : (k + 1) * P],
+                rhs=ident[:],
+                is_transpose=True,
+                start=r == 0,
+                stop=r == TOP - 2,
+            )
+
+        def turn_back(k):
+            turned = keep.tile([P, P], F32, name="turned%d" % k)
+            nc.scalar.copy(turned[:], sums_t[k][:, 0:P])
+            nc.tensor.transpose((back_a if k < 3 else back_b)[:, k % 3 * P : (k % 3 + 1) * P], turned[:], ident[:])
+
+        for r in range(TOP - 2):
+            fetch(r, 0, T)
+            for k in range(blocks):
+                add_turned(r, k)
+        for h in range(2):
+            fetch(TOP - 2, h * 384, (h + 1) * 384)
+            for k in range(3 * h, 3 * h + 3):
+                add_turned(TOP - 2, k)
+            for k in range(3 * h, 3 * h + 3):
+                turn_back(k)
+        fetch(3, 0, T)
+        for t0, t1, back in ((0, 384, back_a), (384, 640, back_b), (640, 768, back_b)):
+            res = keep.tile([P, t1 - t0], F32, name="res%d" % t0)
+            o = t0 % 384
+            nc.vector.tensor_tensor(res[:], back[:, o : o + t1 - t0], prods[3][:, t0:t1], ADD)
+            nc.sync.dma_start(out=out[:, t0:t1], in_=res[:])

@@ -20,7 +20,8 @@ FP4X4 = mybir.dt.float4_e2m1fn_x4
 ADD, MULT, MAX = mybir.AluOpType.add, mybir.AluOpType.mult, mybir.AluOpType.max
 RELU = mybir.ActivationFunctionType.Relu
 
-X_CUTS = (0, 256, 512, 640, 768)
+X_CUTS = (0, 512, 768)
+X_GROUPS = ((0, 256, 160), (256, 512, 160), (512, 768, 160))
 WINDOW = 2048
 GROUP = 8
 W_LOAD = 8
@@ -81,20 +82,16 @@ def tile_moe_tk_lin_relu_kernel(
 
         x_words = keep.tile([P, WINDOW], U32, align_bytes=64, name="x_words")
 
-        def interleave(i, grouped, o):
-            width = X_CUTS[i + 1] - X_CUTS[i]
-            share = width * 5 // 8
-            source = raws[i][:].rearrange("p j w -> p w j")
-            nc.scalar.copy(out=grouped[:, o + share : o + width, :], in_=source[:, share:width, :])
-            nc.vector.tensor_copy(out=grouped[:, o : o + share, :], in_=source[:, 0:share, :])
-
-        for q, parts in enumerate(((0,), (1,), (2, 3))):
-            grouped = keep.tile([P, 256, PACK], BF16, align_bytes=64, name="grouped%d" % q)
-            for i in parts:
-                interleave(i, grouped, X_CUTS[i] - 256 * q)
+        for t0, t1, share in X_GROUPS:
+            i = max(c for c in range(len(raws)) if X_CUTS[c] <= t0)
+            source = raws[i][:, :, t0 - X_CUTS[i] : t1 - X_CUTS[i]].rearrange("p j (c i) -> p c j i", i=4)
+            grouped = keep.tile([P, t1 - t0, PACK], BF16, align_bytes=64, name="grouped%d" % t0)
+            target = grouped[:].rearrange("p (c i) j -> p c j i", i=4)
+            nc.scalar.copy(out=target[:, share // 4 :], in_=source[:, share // 4 :])
+            nc.vector.tensor_copy(out=target[:, : share // 4], in_=source[:, : share // 4])
             nc.vector.quantize_mx(
-                out=x_words[:, 256 * q : 256 * (q + 1)].bitcast(FP8X4),
-                scales=x_bytes[:, 256 * q : 256 * (q + 1)],
+                out=x_words[:, t0:t1].bitcast(FP8X4),
+                scales=x_bytes[:, t0:t1],
                 in_=grouped[:].rearrange("p w j -> p (w j)"),
             )
 

@@ -20,9 +20,9 @@ FP4X4 = mybir.dt.float4_e2m1fn_x4
 ADD, MULT, MAX = mybir.AluOpType.add, mybir.AluOpType.mult, mybir.AluOpType.max
 RELU = mybir.ActivationFunctionType.Relu
 
-X_CUTS = (0, 512, 768)
-X_GROUPS = ((0, 256, 160), (256, 512, 160), (512, 768, 160))
-WINDOW = 2048
+X_CUTS = (0, 256, 512, 640, 768)
+X_GROUPS = ((0, 256, 160), (256, 512, 160), (512, 640, 80), (640, 768, 80))
+WINDOW = 4096
 GROUP = 8
 W_LOAD = 8
 
@@ -84,11 +84,11 @@ def tile_moe_tk_lin_relu_kernel(
 
         for t0, t1, share in X_GROUPS:
             i = max(c for c in range(len(raws)) if X_CUTS[c] <= t0)
-            source = raws[i][:, :, t0 - X_CUTS[i] : t1 - X_CUTS[i]].rearrange("p j (c i) -> p c j i", i=4)
+            source = raws[i][:, :, t0 - X_CUTS[i] : t1 - X_CUTS[i]].rearrange("p j (c i) -> p c j i", i=2)
             grouped = keep.tile([P, t1 - t0, PACK], BF16, align_bytes=64, name="grouped%d" % t0)
-            target = grouped[:].rearrange("p (c i) j -> p c j i", i=4)
-            nc.scalar.copy(out=target[:, share // 4 :], in_=source[:, share // 4 :])
-            nc.vector.tensor_copy(out=target[:, : share // 4], in_=source[:, : share // 4])
+            target = grouped[:].rearrange("p (c i) j -> p c j i", i=2)
+            nc.scalar.copy(out=target[:, share // 2 :], in_=source[:, share // 2 :])
+            nc.vector.tensor_copy(out=target[:, : share // 2], in_=source[:, : share // 2])
             nc.vector.quantize_mx(
                 out=x_words[:, t0:t1].bitcast(FP8X4),
                 scales=x_bytes[:, t0:t1],
@@ -126,7 +126,7 @@ def tile_moe_tk_lin_relu_kernel(
 
         def gather_planes(e0, n):
             planes = keep.tile([P, n * C], U8, align_bytes=64, name="planes%d" % e0)
-            window = x_bytes[:, 0:1024] if n == 1 else x_bytes[:]
+            window = x_bytes[:, 0:1024] if n < 4 else x_bytes[:]
             nc.vector.tensor_copy(planes[:], window.indirect(offs_t[:, e0 * C // 16 : (e0 + n) * C // 16]))
             return planes
 
@@ -139,20 +139,21 @@ def tile_moe_tk_lin_relu_kernel(
                 expert(e0 + i, words[:, i * C :], planes[:, i * C :], 0, acc, i * C)
             return acc
 
-        for e0 in range(0, E, GROUP):
-            words = gather_words(e0, GROUP)
+        for e0, n_words, byte_gathers in ((0, 14, ((4, 4, 4, 2),)), (14, 10, ((3, 3), (1, 1, 1), (1,)))):
+            words = gather_words(e0, n_words)
             first = e0
-            for n in (8,) if e0 + GROUP < E else (4, 2, 1, 1):
-                planes = gather_planes(first, n)
-                m = min(4, n)
-                for h in range(0, n, m):
+            for banks in byte_gathers:
+                planes = gather_planes(first, sum(banks))
+                h = 0
+                for m in banks:
                     acc = experts(first + h, m, words[:, (first + h - e0) * C :], planes[:, h * C :])
                     for i in range(m):
                         if first + h + i < E - 2:
                             relu_scalar(first + h + i, acc, i * C)
                         else:
                             relu_vector(first + h + i, acc, i * C)
-                first += n
+                    h = h + m
+                first += sum(banks)
 
         prods = []
         for r in range(TOP):

@@ -21,7 +21,7 @@ ADD, MULT, MAX = mybir.AluOpType.add, mybir.AluOpType.mult, mybir.AluOpType.max
 RELU = mybir.ActivationFunctionType.Relu
 
 X_CUTS = (0, 256, 512, 640, 768)
-X_GROUPS = ((0, 256, 160), (256, 512, 160), (512, 640, 80), (640, 768, 80))
+X_GROUPS = ((0, 256, 128), (256, 512, 128), (512, 640, 64), (640, 768, 80))
 WINDOW = 4096
 GROUP = 8
 W_LOAD = 8
@@ -39,10 +39,6 @@ def tile_moe_tk_lin_relu_kernel(
         nc.gpsimd.memset(x_bytes[:, 0:T], 0)
         w_planes = keep.tile([P, E, N], U8, align_bytes=64, name="w_planes")
         nc.vector.memset(w_planes[:].rearrange("p e n -> p (e n)").bitcast(I32), 0)
-        warm = keep.tile([P, 8], F32, name="warm")
-        nc.vector.memset(warm[:], 0.0)
-        warm_out = keep.tile([P, 8], F32, name="warm_out")
-        nc.scalar.activation(warm_out[:], warm[:], RELU)
 
         ident = keep.tile([P, P], F32, name="ident")
         make_identity(nc, ident[:])
@@ -87,7 +83,8 @@ def tile_moe_tk_lin_relu_kernel(
             source = raws[i][:, :, t0 - X_CUTS[i] : t1 - X_CUTS[i]].rearrange("p j (c i) -> p c j i", i=2)
             grouped = keep.tile([P, t1 - t0, PACK], BF16, align_bytes=64, name="grouped%d" % t0)
             target = grouped[:].rearrange("p (c i) j -> p c j i", i=2)
-            nc.scalar.copy(out=target[:, share // 2 :], in_=source[:, share // 2 :])
+            if share < t1 - t0:
+                nc.scalar.copy(out=target[:, share // 2 :], in_=source[:, share // 2 :])
             nc.vector.tensor_copy(out=target[:, : share // 2], in_=source[:, : share // 2])
             nc.vector.quantize_mx(
                 out=x_words[:, t0:t1].bitcast(FP8X4),
@@ -139,7 +136,7 @@ def tile_moe_tk_lin_relu_kernel(
                 expert(e0 + i, words[:, i * C :], planes[:, i * C :], 0, acc, i * C)
             return acc
 
-        for e0, n_words, byte_gathers in ((0, 14, ((4, 4, 4, 2),)), (14, 10, ((3, 3), (1, 1, 1), (1,)))):
+        for e0, n_words, byte_gathers in ((0, 15, ((2, 4, 4, 4, 1),)), (15, 9, ((2, 3), (1, 1, 1), (1,)))):
             words = gather_words(e0, n_words)
             first = e0
             for banks in byte_gathers:

@@ -20,11 +20,25 @@ FP4X4 = mybir.dt.float4_e2m1fn_x4
 ADD, MULT, MAX = mybir.AluOpType.add, mybir.AluOpType.mult, mybir.AluOpType.max
 RELU = mybir.ActivationFunctionType.Relu
 
-X_CUTS = (0, 256, 512, 640, 768)
-X_GROUPS = ((0, 256, 128), (256, 512, 128), (512, 640, 64), (640, 768, 80))
+LANES = 16
+BANKS = 8
+BANK = 512
+
+X_LOADS = ((0, 256, 160), (256, 512, 160), (512, 640, 80), (640, 768, 80))
+
 WINDOW = 4096
-GROUP = 8
+SHORT_WINDOW = 1024
+SHORT_GATHER = 4
+
+GATHERS = (
+    ((2, 4, 4, 4, 1),),
+    ((1, 2, 2), (1, 1, 1), (1,)),
+)
+VECTOR_EXPERTS = 2
+
 W_LOAD = 8
+HALF = T // 2
+STORES = ((0, 384), (384, 640), (640, 768))
 
 
 def tile_moe_tk_lin_relu_kernel(
@@ -35,25 +49,30 @@ def tile_moe_tk_lin_relu_kernel(
         keep = ctx.enter_context(tc.tile_pool(name="keep", bufs=1))
         psum = ctx.enter_context(tc.psum_pool(name="psum", bufs=1))
 
+        warm = keep.tile([P, 8], F32, name="warm")
+        nc.gpsimd.memset(warm[:], 0.0)
+        warm_out = keep.tile([P, 8], F32, name="warm_out")
+        nc.scalar.activation(warm_out[:], warm[:], RELU)
+
         x_bytes = keep.tile([P, WINDOW], U8, align_bytes=64, name="x_bytes")
         nc.gpsimd.memset(x_bytes[:, 0:T], 0)
-        w_planes = keep.tile([P, E, N], U8, align_bytes=64, name="w_planes")
-        nc.vector.memset(w_planes[:].rearrange("p e n -> p (e n)").bitcast(I32), 0)
+        w_bytes = keep.tile([P, E, N], U8, align_bytes=64, name="w_bytes")
+        nc.vector.memset(w_bytes[:].rearrange("p e n -> p (e n)").bitcast(I32), 0)
 
         ident = keep.tile([P, P], F32, name="ident")
         make_identity(nc, ident[:])
 
         x_view = xT.rearrange("(p j) w -> p j w", j=PACK)
         raws = []
-        for t0, t1 in zip(X_CUTS[:-1], X_CUTS[1:]):
+        for t0, t1, share in X_LOADS:
             raw = keep.tile([P, PACK, t1 - t0], F32, name="raw%d" % t0)
             nc.sync.dma_start(out=raw[:], in_=x_view[:, :, t0:t1])
             raws.append(raw)
-        offs_t = keep.tile([P, S // 16], U16, name="offs_t")
+        offs_t = keep.tile([P, S // LANES], U16, name="offs_t")
         nc.sync.dma_start(offs_t[:], offs)
         for q in range(4):
             nc.sync.dma_start(
-                out=w_planes[32 * q : 32 * q + 4, :, :].bitcast(I32),
+                out=w_bytes[32 * q : 32 * q + 4, :, :].bitcast(I32),
                 in_=w_scales[:, 0, 4 * q : 4 * q + 4, :].rearrange("e q n -> q e n").bitcast(I32),
             )
         bias = keep.tile([P, E], F32, name="bias")
@@ -68,7 +87,7 @@ def tile_moe_tk_lin_relu_kernel(
             ws.append(w)
         pos_ts, gates = [], []
         for r, pos in enumerate((pos1, pos2, pos3, pos4)):
-            pos_t = keep.tile([P, T // 16], U16, name="pos_t%d" % r)
+            pos_t = keep.tile([P, T // LANES], U16, name="pos_t%d" % r)
             nc.sync.dma_start(pos_t[:], pos)
             pos_ts.append(pos_t)
         for r in range(TOP):
@@ -77,14 +96,11 @@ def tile_moe_tk_lin_relu_kernel(
             gates.append(g)
 
         x_words = keep.tile([P, WINDOW], U32, align_bytes=64, name="x_words")
-
-        for t0, t1, share in X_GROUPS:
-            i = max(c for c in range(len(raws)) if X_CUTS[c] <= t0)
-            source = raws[i][:, :, t0 - X_CUTS[i] : t1 - X_CUTS[i]].rearrange("p j (c i) -> p c j i", i=2)
+        for raw, (t0, t1, share) in zip(raws, X_LOADS):
+            source = raw[:].rearrange("p j (c i) -> p c j i", i=2)
             grouped = keep.tile([P, t1 - t0, PACK], BF16, align_bytes=64, name="grouped%d" % t0)
             target = grouped[:].rearrange("p (c i) j -> p c j i", i=2)
-            if share < t1 - t0:
-                nc.scalar.copy(out=target[:, share // 2 :], in_=source[:, share // 2 :])
+            nc.scalar.copy(out=target[:, share // 2 :], in_=source[:, share // 2 :])
             nc.vector.tensor_copy(out=target[:, : share // 2], in_=source[:, : share // 2])
             nc.vector.quantize_mx(
                 out=x_words[:, t0:t1].bitcast(FP8X4),
@@ -94,85 +110,60 @@ def tile_moe_tk_lin_relu_kernel(
 
         y = keep.tile([P, S], F32, name="y")
 
-        def expert(e, words, planes, col, acc, acc_col):
-            w = ws[e // W_LOAD]
-            nc.tensor.matmul_mx(
-                out=acc[:, acc_col : acc_col + C],
-                lhsT=w[:, e % W_LOAD, :].bitcast(FP4X4),
-                lhsT_scale=w_planes[:, e, :],
-                rhs=words[:, col : col + C].bitcast(FP8X4),
-                rhs_scale=planes[:, col : col + C],
-                start=True,
-                stop=True,
-            )
+        def slots(e0, n):
+            return offs_t[:, e0 * C // LANES : (e0 + n) * C // LANES]
 
-        def relu_scalar(e, acc, acc_col):
-            nc.scalar.activation(
-                y[:, e * C : (e + 1) * C], acc[:, acc_col : acc_col + C], RELU, bias=bias[:, e : e + 1]
-            )
-
-        def relu_vector(e, acc, acc_col):
-            nc.vector.tensor_scalar(
-                y[:, e * C : (e + 1) * C], acc[:, acc_col : acc_col + C], bias[:, e : e + 1], 0.0, op0=ADD, op1=MAX
-            )
-
-        def gather_words(e0, n):
-            words = keep.tile([P, n * C], U32, align_bytes=64, name="words%d" % e0)
-            nc.vector.tensor_copy(words[:], x_words[:].indirect(offs_t[:, e0 * C // 16 : (e0 + n) * C // 16]))
-            return words
-
-        def gather_planes(e0, n):
-            planes = keep.tile([P, n * C], U8, align_bytes=64, name="planes%d" % e0)
-            window = x_bytes[:, 0:1024] if n < 4 else x_bytes[:]
-            nc.vector.tensor_copy(planes[:], window.indirect(offs_t[:, e0 * C // 16 : (e0 + n) * C // 16]))
-            return planes
-
-        banks_used = []
-
-        def experts(e0, n, words, planes):
-            acc = psum.tile([P, 512], F32, name="bank%d" % (len(banks_used) % 8))
-            banks_used.append(e0)
-            for i in range(n):
-                expert(e0 + i, words[:, i * C :], planes[:, i * C :], 0, acc, i * C)
-            return acc
-
-        for e0, n_words, byte_gathers in ((0, 15, ((2, 4, 4, 4, 1),)), (15, 9, ((2, 3), (1, 1, 1), (1,)))):
-            words = gather_words(e0, n_words)
-            first = e0
+        e = 0
+        bank = 0
+        for byte_gathers in GATHERS:
+            words_from = e
+            n_words = sum(sum(banks) for banks in byte_gathers)
+            words = keep.tile([P, n_words * C], U32, align_bytes=64, name="words%d" % e)
+            nc.vector.tensor_copy(words[:], x_words[:].indirect(slots(e, n_words)))
             for banks in byte_gathers:
-                planes = gather_planes(first, sum(banks))
-                h = 0
-                for m in banks:
-                    acc = experts(first + h, m, words[:, (first + h - e0) * C :], planes[:, h * C :])
-                    for i in range(m):
-                        if first + h + i < E - 2:
-                            relu_scalar(first + h + i, acc, i * C)
+                bytes_from = e
+                scales = keep.tile([P, sum(banks) * C], U8, align_bytes=64, name="scales%d" % e)
+                window = x_bytes[:, 0:SHORT_WINDOW] if sum(banks) < SHORT_GATHER else x_bytes[:]
+                nc.vector.tensor_copy(scales[:], window.indirect(slots(e, sum(banks))))
+                for n in banks:
+                    acc = psum.tile([P, BANK], F32, name="bank%d" % (bank % BANKS))
+                    bank = bank + 1
+                    for i in range(n):
+                        wc, bc = (e + i - words_from) * C, (e + i - bytes_from) * C
+                        nc.tensor.matmul_mx(
+                            out=acc[:, i * C : (i + 1) * C],
+                            lhsT=ws[(e + i) // W_LOAD][:, (e + i) % W_LOAD, :].bitcast(FP4X4),
+                            lhsT_scale=w_bytes[:, e + i, :],
+                            rhs=words[:, wc : wc + C].bitcast(FP8X4),
+                            rhs_scale=scales[:, bc : bc + C],
+                            start=True,
+                            stop=True,
+                        )
+                    for i in range(n):
+                        dst = y[:, (e + i) * C : (e + i + 1) * C]
+                        src = acc[:, i * C : (i + 1) * C]
+                        column = bias[:, e + i : e + i + 1]
+                        if e + i < E - VECTOR_EXPERTS:
+                            nc.scalar.activation(dst, src, RELU, bias=column)
                         else:
-                            relu_vector(first + h + i, acc, i * C)
-                    h = h + m
-                first += sum(banks)
+                            nc.vector.tensor_scalar(dst, src, column, 0.0, op0=ADD, op1=MAX)
+                    e = e + n
 
-        prods = []
-        for r in range(TOP):
-            prod = keep.tile([P, T], F32, name="prod%d" % r)
-            prods.append(prod)
+        prods = [keep.tile([P, T], F32, name="prod%d" % r) for r in range(TOP)]
 
-        def fetch(r, lo, hi):
+        def fetch(r, t0, t1):
             nc.vector.tensor_tensor(
-                prods[r][:, lo:hi], y[:].indirect(pos_ts[r][:, lo // 16 : hi // 16]), gates[r][:, lo:hi], MULT
+                prods[r][:, t0:t1], y[:].indirect(pos_ts[r][:, t0 // LANES : t1 // LANES]), gates[r][:, t0:t1], MULT
             )
 
         blocks = T // P
-        sums_t = []
-        for k in range(blocks):
-            sum_t = psum.tile([P, 512], F32, name="bank%d" % k)
-            sums_t.append(sum_t)
-        back_a = psum.tile([P, 512], F32, name="bank6")
-        back_b = psum.tile([P, 512], F32, name="bank7")
+        per_half = HALF // P
+        sums = [psum.tile([P, BANK], F32, name="bank%d" % k) for k in range(blocks)]
+        backs = [psum.tile([P, BANK], F32, name="bank%d" % (blocks + h)) for h in range(2)]
 
         def add_turned(r, k):
             nc.tensor.matmul(
-                out=sums_t[k][:, 0:P],
+                out=sums[k][:, 0:P],
                 lhsT=prods[r][:, k * P : (k + 1) * P],
                 rhs=ident[:],
                 is_transpose=True,
@@ -182,22 +173,23 @@ def tile_moe_tk_lin_relu_kernel(
 
         def turn_back(k):
             turned = keep.tile([P, P], F32, name="turned%d" % k)
-            nc.scalar.copy(turned[:], sums_t[k][:, 0:P])
-            nc.tensor.transpose((back_a if k < 3 else back_b)[:, k % 3 * P : (k % 3 + 1) * P], turned[:], ident[:])
+            nc.scalar.copy(turned[:], sums[k][:, 0:P])
+            o = k % per_half * P
+            nc.tensor.transpose(backs[k // per_half][:, o : o + P], turned[:], ident[:])
 
         for r in range(TOP - 2):
             fetch(r, 0, T)
             for k in range(blocks):
                 add_turned(r, k)
         for h in range(2):
-            fetch(TOP - 2, h * 384, (h + 1) * 384)
-            for k in range(3 * h, 3 * h + 3):
+            fetch(TOP - 2, h * HALF, (h + 1) * HALF)
+            for k in range(per_half * h, per_half * (h + 1)):
                 add_turned(TOP - 2, k)
-            for k in range(3 * h, 3 * h + 3):
+            for k in range(per_half * h, per_half * (h + 1)):
                 turn_back(k)
-        fetch(3, 0, T)
-        for t0, t1, back in ((0, 384, back_a), (384, 640, back_b), (640, 768, back_b)):
+        fetch(TOP - 1, 0, T)
+        for t0, t1 in STORES:
             res = keep.tile([P, t1 - t0], F32, name="res%d" % t0)
-            o = t0 % 384
-            nc.vector.tensor_tensor(res[:], back[:, o : o + t1 - t0], prods[3][:, t0:t1], ADD)
+            o = t0 % HALF
+            nc.vector.tensor_tensor(res[:], backs[t0 // HALF][:, o : o + t1 - t0], prods[TOP - 1][:, t0:t1], ADD)
             nc.sync.dma_start(out=out[:, t0:t1], in_=res[:])

@@ -50,7 +50,7 @@ def tile_moe_tk_lin_relu_kernel(
         psum = ctx.enter_context(tc.psum_pool(name="psum", bufs=1))
 
         warm = keep.tile([P, 8], F32, name="warm")
-        nc.gpsimd.memset(warm[:], 0.0)
+        nc.vector.memset(warm[:], 0.0)
         warm_out = keep.tile([P, 8], F32, name="warm_out")
         nc.scalar.activation(warm_out[:], warm[:], RELU)
 
@@ -151,10 +151,8 @@ def tile_moe_tk_lin_relu_kernel(
 
         prods = [keep.tile([P, T], F32, name="prod%d" % r) for r in range(TOP)]
 
-        def fetch(r, t0, t1):
-            nc.vector.tensor_tensor(
-                prods[r][:, t0:t1], y[:].indirect(pos_ts[r][:, t0 // LANES : t1 // LANES]), gates[r][:, t0:t1], MULT
-            )
+        def fetch(r):
+            nc.vector.tensor_tensor(prods[r][:], y[:].indirect(pos_ts[r][:]), gates[r][:], MULT)
 
         blocks = T // P
         per_half = HALF // P
@@ -177,17 +175,13 @@ def tile_moe_tk_lin_relu_kernel(
             o = k % per_half * P
             nc.tensor.transpose(backs[k // per_half][:, o : o + P], turned[:], ident[:])
 
-        for r in range(TOP - 2):
-            fetch(r, 0, T)
+        for r in range(TOP - 1):
+            fetch(r)
             for k in range(blocks):
                 add_turned(r, k)
-        for h in range(2):
-            fetch(TOP - 2, h * HALF, (h + 1) * HALF)
-            for k in range(per_half * h, per_half * (h + 1)):
-                add_turned(TOP - 2, k)
-            for k in range(per_half * h, per_half * (h + 1)):
-                turn_back(k)
-        fetch(TOP - 1, 0, T)
+        for k in range(blocks):
+            turn_back(k)
+        fetch(TOP - 1)
         for t0, t1 in STORES:
             res = keep.tile([P, t1 - t0], F32, name="res%d" % t0)
             o = t0 % HALF

@@ -24,7 +24,8 @@ LANES = 16
 BANKS = 8
 BANK = 512
 
-X_LOADS = ((0, 256, 160), (256, 512, 160), (512, 640, 80), (640, 768, 80))
+X_LOADS = ((256, 128), (256,), (128,))
+VECTOR_EIGHTHS = 5
 
 WINDOW = 4096
 SHORT_WINDOW = 1024
@@ -64,10 +65,15 @@ def tile_moe_tk_lin_relu_kernel(
 
         x_view = xT.rearrange("(p j) w -> p j w", j=PACK)
         raws = []
-        for t0, t1, share in X_LOADS:
-            raw = keep.tile([P, PACK, t1 - t0], F32, name="raw%d" % t0)
-            nc.sync.dma_start(out=raw[:], in_=x_view[:, :, t0:t1])
-            raws.append(raw)
+        t0 = 0
+        for widths in X_LOADS:
+            raw = keep.tile([P, PACK, sum(widths)], F32, name="raw%d" % t0)
+            nc.sync.dma_start(out=raw[:], in_=x_view[:, :, t0 : t0 + sum(widths)])
+            o = 0
+            for width in widths:
+                raws.append((raw[:, :, o : o + width], t0 + o, t0 + o + width))
+                o = o + width
+            t0 = t0 + o
         offs_t = keep.tile([P, S // LANES], U16, name="offs_t")
         nc.sync.dma_start(offs_t[:], offs)
         for q in range(4):
@@ -96,8 +102,9 @@ def tile_moe_tk_lin_relu_kernel(
             gates.append(g)
 
         x_words = keep.tile([P, WINDOW], U32, align_bytes=64, name="x_words")
-        for raw, (t0, t1, share) in zip(raws, X_LOADS):
-            source = raw[:].rearrange("p j (c i) -> p c j i", i=2)
+        for raw, t0, t1 in raws:
+            share = (t1 - t0) * VECTOR_EIGHTHS // 8
+            source = raw.rearrange("p j (c i) -> p c j i", i=2)
             grouped = keep.tile([P, t1 - t0, PACK], BF16, align_bytes=64, name="grouped%d" % t0)
             target = grouped[:].rearrange("p (c i) j -> p c j i", i=2)
             nc.scalar.copy(out=target[:, share // 2 :], in_=source[:, share // 2 :])

@@ -38,8 +38,8 @@ GATHERS = (
 VECTOR_EXPERTS = 2
 
 W_LOAD = 8
-HALF = T // 2
-STORES = ((0, 384), (384, 640), (640, 768))
+RANGE = 256
+STORES = ((0, 256), (256, 512), (512, 640), (640, 768))
 
 
 def tile_moe_tk_lin_relu_kernel(
@@ -150,7 +150,7 @@ def tile_moe_tk_lin_relu_kernel(
                         dst = y[:, (e + i) * C : (e + i + 1) * C]
                         src = acc[:, i * C : (i + 1) * C]
                         column = bias[:, e + i : e + i + 1]
-                        if e + i < E - VECTOR_EXPERTS:
+                        if not E - 1 - VECTOR_EXPERTS <= e + i < E - 1:
                             nc.scalar.activation(dst, src, RELU, bias=column)
                         else:
                             nc.vector.tensor_scalar(dst, src, column, 0.0, op0=ADD, op1=MAX)
@@ -158,39 +158,39 @@ def tile_moe_tk_lin_relu_kernel(
 
         prods = [keep.tile([P, T], F32, name="prod%d" % r) for r in range(TOP)]
 
-        def fetch(r):
-            nc.vector.tensor_tensor(prods[r][:], y[:].indirect(pos_ts[r][:]), gates[r][:], MULT)
+        def fetch(r, t0, t1):
+            entries = pos_ts[r][:, t0 // LANES : t1 // LANES]
+            nc.vector.tensor_tensor(prods[r][:, t0:t1], y[:].indirect(entries), gates[r][:, t0:t1], MULT)
 
-        blocks = T // P
-        per_half = HALF // P
-        sums = [psum.tile([P, BANK], F32, name="bank%d" % k) for k in range(blocks)]
-        backs = [psum.tile([P, BANK], F32, name="bank%d" % (blocks + h)) for h in range(2)]
-
-        def add_turned(r, k):
-            nc.tensor.matmul(
-                out=sums[k][:, 0:P],
-                lhsT=prods[r][:, k * P : (k + 1) * P],
-                rhs=ident[:],
-                is_transpose=True,
-                start=r == 0,
-                stop=r == TOP - 2,
-            )
-
-        def turn_back(k):
-            turned = keep.tile([P, P], F32, name="turned%d" % k)
-            nc.scalar.copy(turned[:], sums[k][:, 0:P])
-            o = k % per_half * P
-            nc.tensor.transpose(backs[k // per_half][:, o : o + P], turned[:], ident[:])
-
+        ranges, per_range = T // RANGE, RANGE // P
+        sums = [psum.tile([P, BANK], F32, name="bank%d" % j) for j in range(ranges)]
+        backs = [psum.tile([P, BANK], F32, name="bank%d" % (ranges + j)) for j in range(ranges)]
         for r in range(TOP - 1):
-            fetch(r)
-            for k in range(blocks):
-                add_turned(r, k)
-        for k in range(blocks):
-            turn_back(k)
-        fetch(TOP - 1)
+            for j in range(ranges):
+                if r < TOP - 2 and j == 0:
+                    fetch(r, 0, T)
+                if r == TOP - 2 and j < 2:
+                    fetch(r, j * RANGE, T if j else RANGE)
+                for i in range(per_range):
+                    k = j * per_range + i
+                    nc.tensor.matmul(
+                        out=sums[j][:, i * P : (i + 1) * P],
+                        lhsT=prods[r][:, k * P : (k + 1) * P],
+                        rhs=ident[:],
+                        is_transpose=True,
+                        start=r == 0 and i == 0,
+                        stop=r == TOP - 2 and i == per_range - 1,
+                    )
+        for j in range(ranges):
+            turned = keep.tile([P, RANGE], F32, name="turned%d" % j)
+            nc.scalar.copy(turned[:], sums[j][:, 0:RANGE])
+            for i in range(per_range):
+                nc.tensor.transpose(backs[j][:, i * P : (i + 1) * P], turned[:, i * P : (i + 1) * P], ident[:])
+        cut = STORES[-1][0]
+        fetch(TOP - 1, 0, cut)
+        fetch(TOP - 1, cut, T)
         for t0, t1 in STORES:
             res = keep.tile([P, t1 - t0], F32, name="res%d" % t0)
-            o = t0 % HALF
-            nc.vector.tensor_tensor(res[:], backs[t0 // HALF][:, o : o + t1 - t0], prods[TOP - 1][:, t0:t1], ADD)
+            o = t0 % RANGE
+            nc.vector.tensor_tensor(res[:], backs[t0 // RANGE][:, o : o + t1 - t0], prods[TOP - 1][:, t0:t1], ADD)
             nc.sync.dma_start(out=out[:, t0:t1], in_=res[:])

@@ -169,8 +169,8 @@ def tile_moe_tk_lin_relu_kernel(
             for j in range(ranges):
                 if r < TOP - 2 and j == 0:
                     fetch(r, 0, T)
-                if r == TOP - 2 and j < 2:
-                    fetch(r, j * RANGE, T if j else RANGE)
+                if r == TOP - 2 and j != 1:
+                    fetch(r, j * RANGE, T if j else 2 * RANGE)
                 for i in range(per_range):
                     k = j * per_range + i
                     nc.tensor.matmul(

@@ -31,10 +31,9 @@ WINDOW = 4096
 SHORT_WINDOW = 1024
 SHORT_GATHER = 4
 
-GATHERS = (
-    ((2, 4, 4, 4, 1),),
-    ((1, 2, 2), (1, 1, 1), (1,)),
-)
+WORDS, SCALES = 0, 1
+GATHERS = ((WORDS, 16), (SCALES, 16), (WORDS, 8), (SCALES, 4), (SCALES, 3), (SCALES, 1))
+PACED_BANKS = 5
 VECTOR_EXPERTS = 2
 
 W_LOAD = 8
@@ -117,44 +116,35 @@ def tile_moe_tk_lin_relu_kernel(
 
         y = keep.tile([P, S], F32, name="y")
 
-        def slots(e0, n):
-            return offs_t[:, e0 * C // LANES : (e0 + n) * C // LANES]
-
-        e = 0
-        bank = 0
-        for byte_gathers in GATHERS:
-            words_from = e
-            n_words = sum(sum(banks) for banks in byte_gathers)
-            words = keep.tile([P, n_words * C], U32, align_bytes=64, name="words%d" % e)
-            nc.vector.tensor_copy(words[:], x_words[:].indirect(slots(e, n_words)))
-            for banks in byte_gathers:
-                bytes_from = e
-                scales = keep.tile([P, sum(banks) * C], U8, align_bytes=64, name="scales%d" % e)
-                window = x_bytes[:, 0:SHORT_WINDOW] if sum(banks) < SHORT_GATHER else x_bytes[:]
-                nc.vector.tensor_copy(scales[:], window.indirect(slots(e, sum(banks))))
-                for n in banks:
-                    acc = psum.tile([P, BANK], F32, name="bank%d" % (bank % BANKS))
-                    bank = bank + 1
-                    for i in range(n):
-                        wc, bc = (e + i - words_from) * C, (e + i - bytes_from) * C
-                        nc.tensor.matmul_mx(
-                            out=acc[:, i * C : (i + 1) * C],
-                            lhsT=ws[(e + i) // W_LOAD][:, (e + i) % W_LOAD, :].bitcast(FP4X4),
-                            lhsT_scale=w_bytes[:, e + i, :],
-                            rhs=words[:, wc : wc + C].bitcast(FP8X4),
-                            rhs_scale=scales[:, bc : bc + C],
-                            start=True,
-                            stop=True,
-                        )
-                    for i in range(n):
-                        dst = y[:, (e + i) * C : (e + i + 1) * C]
-                        src = acc[:, i * C : (i + 1) * C]
-                        column = bias[:, e + i : e + i + 1]
-                        if not E - 1 - VECTOR_EXPERTS <= e + i < E - 1:
-                            nc.scalar.activation(dst, src, RELU, bias=column)
-                        else:
-                            nc.vector.tensor_scalar(dst, src, column, 0.0, op0=ADD, op1=MAX)
-                    e = e + n
+        tables = (x_words, x_bytes)
+        gathered = ([], [])
+        done = 0
+        paced = GATHERS[0][1]
+        for sort, count in GATHERS:
+            first = len(gathered[sort])
+            picked = keep.tile([P, count * C], (U32, U8)[sort], align_bytes=64, name="picked%d_%d" % (sort, first))
+            window = tables[sort][:, 0:SHORT_WINDOW] if count < SHORT_GATHER else tables[sort][:]
+            entries = offs_t[:, first * C // LANES : (first + count) * C // LANES]
+            nc.vector.tensor_copy(picked[:], window.indirect(entries))
+            gathered[sort].extend([picked[:, i * C : (i + 1) * C] for i in range(count)])
+            for e in range(done, min(len(gathered[WORDS]), len(gathered[SCALES]))):
+                bank = e % PACED_BANKS if e < paced else (PACED_BANKS + e - paced) % BANKS
+                acc = psum.tile([P, BANK], F32, name="bank%d" % bank)
+                nc.tensor.matmul_mx(
+                    out=acc[:, 0:C],
+                    lhsT=ws[e // W_LOAD][:, e % W_LOAD, :].bitcast(FP4X4),
+                    lhsT_scale=w_bytes[:, e, :],
+                    rhs=gathered[WORDS][e].bitcast(FP8X4),
+                    rhs_scale=gathered[SCALES][e],
+                    start=True,
+                    stop=True,
+                )
+                dst = y[:, e * C : (e + 1) * C]
+                if E - 1 - VECTOR_EXPERTS <= e < E - 1:
+                    nc.vector.tensor_scalar(dst, acc[:, 0:C], bias[:, e : e + 1], 0.0, op0=ADD, op1=MAX)
+                else:
+                    nc.scalar.activation(dst, acc[:, 0:C], RELU, bias=bias[:, e : e + 1])
+                done = e + 1
 
         prods = [keep.tile([P, T], F32, name="prod%d" % r) for r in range(TOP)]
 

@@ -61,6 +61,9 @@ def tile_moe_tk_lin_relu_kernel(
 
         ident = keep.tile([P, P], F32, name="ident")
         make_identity(nc, ident[:])
+        blocks = T // P
+        gate_rows = keep.tile([P, P], F32, name="gate_rows")
+        nc.gpsimd.memset(gate_rows[:], 0.0)
 
         x_view = xT.rearrange("(p j) w -> p j w", j=PACK)
         raws = []
@@ -75,6 +78,10 @@ def tile_moe_tk_lin_relu_kernel(
             t0 = t0 + o
         offs_t = keep.tile([P, S // LANES], U16, name="offs_t")
         nc.sync.dma_start(offs_t[:], offs)
+        for r in range(TOP):
+            nc.sync.dma_start(
+                out=gate_rows[blocks * r : blocks * (r + 1), :], in_=gate[r, 0, :].rearrange("(k t) -> k t", t=P)
+            )
         for q in range(4):
             nc.sync.dma_start(
                 out=w_bytes[32 * q : 32 * q + 4, :, :].bitcast(I32),
@@ -90,15 +97,11 @@ def tile_moe_tk_lin_relu_kernel(
                 in_=w_words[e0 : e0 + W_LOAD, 0, :, :].rearrange("e p c -> p e c").bitcast(I32),
             )
             ws.append(w)
-        pos_ts, gates = [], []
+        pos_ts = []
         for r, pos in enumerate((pos1, pos2, pos3, pos4)):
             pos_t = keep.tile([P, T // LANES], U16, name="pos_t%d" % r)
             nc.sync.dma_start(pos_t[:], pos)
             pos_ts.append(pos_t)
-        for r in range(TOP):
-            g = keep.tile([P, T], F32, name="gate%d" % r)
-            nc.sync.dma_start(out=g[:], in_=gate[r])
-            gates.append(g)
 
         x_words = keep.tile([P, WINDOW], U32, align_bytes=64, name="x_words")
         for raw, t0, t1 in raws:
@@ -113,6 +116,18 @@ def tile_moe_tk_lin_relu_kernel(
                 scales=x_bytes[:, t0:t1],
                 in_=grouped[:].rearrange("p w j -> p (w j)"),
             )
+
+        turned_rows = psum.tile([P, BANK], F32, name="bank%d" % (BANKS - 1))
+        nc.tensor.transpose(turned_rows[:, 0:P], gate_rows[:], ident[:])
+        gate_cols = keep.tile([P, TOP * blocks], F32, name="gate_cols")
+        nc.scalar.copy(gate_cols[:], turned_rows[:, 0 : TOP * blocks])
+        gates = keep.tile([P, TOP * T], F32, name="gates")
+        for fill in range(TOP * T // BANK):
+            spread = psum.tile([P, BANK], F32, name="bank%d" % (fill % PACED_BANKS))
+            for i in range(BANK // P):
+                c = fill * (BANK // P) + i
+                nc.tensor.transpose(spread[:, i * P : (i + 1) * P], gate_cols[:, c : c + 1].to_broadcast([P, P]), ident[:])
+            nc.scalar.copy(gates[:, fill * BANK : (fill + 1) * BANK], spread[:])
 
         y = keep.tile([P, S], F32, name="y")
 
@@ -150,7 +165,7 @@ def tile_moe_tk_lin_relu_kernel(
 
         def fetch(r, t0, t1):
             entries = pos_ts[r][:, t0 // LANES : t1 // LANES]
-            nc.vector.tensor_tensor(prods[r][:, t0:t1], y[:].indirect(entries), gates[r][:, t0:t1], MULT)
+            nc.vector.tensor_tensor(prods[r][:, t0:t1], y[:].indirect(entries), gates[:, r * T + t0 : r * T + t1], MULT)
 
         ranges, per_range = T // RANGE, RANGE // P
         sums = [psum.tile([P, BANK], F32, name="bank%d" % j) for j in range(ranges)]

@@ -19,6 +19,7 @@ FP8X4 = mybir.dt.float8_e4m3fn_x4
 FP4X4 = mybir.dt.float4_e2m1fn_x4
 ADD, MULT, MAX = mybir.AluOpType.add, mybir.AluOpType.mult, mybir.AluOpType.max
 RELU = mybir.ActivationFunctionType.Relu
+COPY = mybir.ActivationFunctionType.Copy
 
 LANES = 16
 BANKS = 8
@@ -38,7 +39,8 @@ VECTOR_EXPERTS = 2
 
 W_LOAD = 8
 RANGE = 256
-STORES = ((0, 256), (256, 512), (512, 640), (640, 768))
+STORES = ((256, 512), (512, 640), (640, 768))
+OWN = 256
 
 
 def tile_moe_tk_lin_relu_kernel(
@@ -121,13 +123,14 @@ def tile_moe_tk_lin_relu_kernel(
         nc.tensor.transpose(turned_rows[:, 0:P], gate_rows[:], ident[:])
         gate_cols = keep.tile([P, TOP * blocks], F32, name="gate_cols")
         nc.scalar.copy(gate_cols[:], turned_rows[:, 0 : TOP * blocks])
-        gates = keep.tile([P, TOP * T], F32, name="gates")
-        for fill in range(TOP * T // BANK):
-            spread = psum.tile([P, BANK], F32, name="bank%d" % (fill % PACED_BANKS))
-            for i in range(BANK // P):
-                c = fill * (BANK // P) + i
+        rest = T - OWN
+        gates = keep.tile([P, TOP * rest], F32, name="gates")
+        for r in range(TOP):
+            spread = psum.tile([P, BANK], F32, name="bank%d" % r)
+            for i in range(rest // P):
+                c = r * blocks + OWN // P + i
                 nc.tensor.transpose(spread[:, i * P : (i + 1) * P], gate_cols[:, c : c + 1].to_broadcast([P, P]), ident[:])
-            nc.scalar.copy(gates[:, fill * BANK : (fill + 1) * BANK], spread[:])
+            nc.scalar.copy(gates[:, r * rest : (r + 1) * rest], spread[:, 0:rest])
 
         y = keep.tile([P, S], F32, name="y")
 
@@ -161,41 +164,61 @@ def tile_moe_tk_lin_relu_kernel(
                     nc.scalar.activation(dst, acc[:, 0:C], RELU, bias=bias[:, e : e + 1])
                 done = e + 1
 
-        prods = [keep.tile([P, T], F32, name="prod%d" % r) for r in range(TOP)]
+        def turn(dst, src, start, stop):
+            nc.tensor.matmul(out=dst, lhsT=src, rhs=ident[:], is_transpose=True, start=start, stop=stop)
+
+        per_range = RANGE // P
+        prods = [keep.tile([P, rest], F32, name="prod%d" % r) for r in range(TOP)]
 
         def fetch(r, t0, t1):
             entries = pos_ts[r][:, t0 // LANES : t1 // LANES]
-            nc.vector.tensor_tensor(prods[r][:, t0:t1], y[:].indirect(entries), gates[:, r * T + t0 : r * T + t1], MULT)
+            gate_part = gates[:, r * rest + t0 - OWN : r * rest + t1 - OWN]
+            nc.vector.tensor_tensor(prods[r][:, t0 - OWN : t1 - OWN], y[:].indirect(entries), gate_part, MULT)
 
-        ranges, per_range = T // RANGE, RANGE // P
+        ranges = rest // RANGE
         sums = [psum.tile([P, BANK], F32, name="bank%d" % j) for j in range(ranges)]
         backs = [psum.tile([P, BANK], F32, name="bank%d" % (ranges + j)) for j in range(ranges)]
-        for r in range(TOP - 1):
-            for j in range(ranges):
-                if r < TOP - 2 and j == 0:
-                    fetch(r, 0, T)
-                if r == TOP - 2 and j != 1:
-                    fetch(r, j * RANGE, T if j else 2 * RANGE)
-                for i in range(per_range):
-                    k = j * per_range + i
-                    nc.tensor.matmul(
-                        out=sums[j][:, i * P : (i + 1) * P],
-                        lhsT=prods[r][:, k * P : (k + 1) * P],
-                        rhs=ident[:],
-                        is_transpose=True,
-                        start=r == 0 and i == 0,
-                        stop=r == TOP - 2 and i == per_range - 1,
-                    )
+        own_sum = psum.tile([P, BANK], F32, name="bank%d" % (2 * ranges))
+        own_blocks = OWN // P
+        for r in range(TOP):
+            plain = keep.tile([P, OWN], F32, name="plain%d" % r)
+            nc.scalar.activation(plain[:], y[:].indirect(pos_ts[r][:, 0 : OWN // LANES]), COPY)
+            turned_own = psum.tile([P, BANK], F32, name="bank%d" % (2 * ranges + 1 + r % 2))
+            for i in range(own_blocks):
+                turn(turned_own[:, i * P : (i + 1) * P], plain[:, i * P : (i + 1) * P], True, True)
+            if r < TOP - 1:
+                for j in range(ranges):
+                    if r == TOP - 2:
+                        fetch(r, OWN + j * RANGE, OWN + (j + 1) * RANGE)
+                    elif j == 0:
+                        fetch(r, OWN, T)
+                    for i in range(per_range):
+                        k = j * per_range + i
+                        first, last = r == 0 and i == 0, r == TOP - 2 and i == per_range - 1
+                        turn(sums[j][:, i * P : (i + 1) * P], prods[r][:, k * P : (k + 1) * P], first, last)
+            scaled = keep.tile([P, OWN], F32, name="scaled%d" % r)
+            for i in range(own_blocks):
+                c = r * blocks + i
+                nc.scalar.activation(
+                    scaled[:, i * P : (i + 1) * P], turned_own[:, i * P : (i + 1) * P], COPY, scale=gate_cols[:, c : c + 1]
+                )
+            for i in range(own_blocks):
+                first, last = r == 0 and i == 0, r == TOP - 1 and i == own_blocks - 1
+                turn(own_sum[:, i * P : (i + 1) * P], scaled[:, i * P : (i + 1) * P], first, last)
         for j in range(ranges):
             turned = keep.tile([P, RANGE], F32, name="turned%d" % j)
             nc.scalar.copy(turned[:], sums[j][:, 0:RANGE])
             for i in range(per_range):
-                nc.tensor.transpose(backs[j][:, i * P : (i + 1) * P], turned[:, i * P : (i + 1) * P], ident[:])
+                turn(backs[j][:, i * P : (i + 1) * P], turned[:, i * P : (i + 1) * P], True, True)
+        own_res = keep.tile([P, OWN], F32, name="own_res")
+        nc.scalar.copy(own_res[:], own_sum[:, 0:OWN])
+        nc.sync.dma_start(out=out[:, 0:OWN], in_=own_res[:])
         cut = STORES[-1][0]
-        fetch(TOP - 1, 0, cut)
+        fetch(TOP - 1, OWN, cut)
         fetch(TOP - 1, cut, T)
         for t0, t1 in STORES:
             res = keep.tile([P, t1 - t0], F32, name="res%d" % t0)
             o = t0 % RANGE
-            nc.vector.tensor_tensor(res[:], backs[t0 // RANGE][:, o : o + t1 - t0], prods[TOP - 1][:, t0:t1], ADD)
+            back = backs[(t0 - OWN) // RANGE]
+            nc.vector.tensor_tensor(res[:], back[:, o : o + t1 - t0], prods[TOP - 1][:, t0 - OWN : t1 - OWN], ADD)
             nc.sync.dma_start(out=out[:, t0:t1], in_=res[:])

@@ -39,7 +39,6 @@ VECTOR_EXPERTS = 2
 
 W_LOAD = 8
 RANGE = 256
-STORES = ((256, 512), (512, 640), (640, 768))
 OWN = 256
 
 
@@ -167,58 +166,57 @@ def tile_moe_tk_lin_relu_kernel(
         def turn(dst, src, start, stop):
             nc.tensor.matmul(out=dst, lhsT=src, rhs=ident[:], is_transpose=True, start=start, stop=stop)
 
-        per_range = RANGE // P
-        prods = [keep.tile([P, rest], F32, name="prod%d" % r) for r in range(TOP)]
-
         def fetch(r, t0, t1):
+            prod = keep.tile([P, t1 - t0], F32, name="prod%d_%d" % (r, t0))
             entries = pos_ts[r][:, t0 // LANES : t1 // LANES]
             gate_part = gates[:, r * rest + t0 - OWN : r * rest + t1 - OWN]
-            nc.vector.tensor_tensor(prods[r][:, t0 - OWN : t1 - OWN], y[:].indirect(entries), gate_part, MULT)
+            nc.vector.tensor_tensor(prod[:], y[:].indirect(entries), gate_part, MULT)
+            return prod
 
-        ranges = rest // RANGE
-        sums = [psum.tile([P, BANK], F32, name="bank%d" % j) for j in range(ranges)]
-        backs = [psum.tile([P, BANK], F32, name="bank%d" % (ranges + j)) for j in range(ranges)]
-        own_sum = psum.tile([P, BANK], F32, name="bank%d" % (2 * ranges))
-        own_blocks = OWN // P
+        def store(t0, bank):
+            res = keep.tile([P, RANGE], F32, name="res%d" % t0)
+            nc.scalar.copy(res[:], bank[:, 0:RANGE])
+            nc.scalar.dma_start(out=out[:, t0 : t0 + RANGE], in_=res[:])
+
+        per_range = RANGE // P
+        halves = [slice(i * P, (i + 1) * P) for i in range(per_range)]
+        mid_sum = psum.tile([P, BANK], F32, name="bank0")
+        own_sum = psum.tile([P, BANK], F32, name="bank1")
+        mid_back = psum.tile([P, BANK], F32, name="bank2")
+        turned_own = []
         for r in range(TOP):
             plain = keep.tile([P, OWN], F32, name="plain%d" % r)
             nc.scalar.activation(plain[:], y[:].indirect(pos_ts[r][:, 0 : OWN // LANES]), COPY)
-            turned_own = psum.tile([P, BANK], F32, name="bank%d" % (2 * ranges + 1 + r % 2))
-            for i in range(own_blocks):
-                turn(turned_own[:, i * P : (i + 1) * P], plain[:, i * P : (i + 1) * P], True, True)
-            if r < TOP - 1:
-                for j in range(ranges):
-                    if r == TOP - 2:
-                        fetch(r, OWN + j * RANGE, OWN + (j + 1) * RANGE)
-                    elif j == 0:
-                        fetch(r, OWN, T)
-                    for i in range(per_range):
-                        k = j * per_range + i
-                        first, last = r == 0 and i == 0, r == TOP - 2 and i == per_range - 1
-                        turn(sums[j][:, i * P : (i + 1) * P], prods[r][:, k * P : (k + 1) * P], first, last)
+            turned_own.append(psum.tile([P, BANK], F32, name="bank%d" % (3 + r)))
+            for h in halves:
+                turn(turned_own[r][:, h], plain[:, h], True, True)
+            prod = fetch(r, OWN, OWN + RANGE)
+            for i, h in enumerate(halves):
+                turn(mid_sum[:, h], prod[:, h], r == 0 and i == 0, r == TOP - 1 and i == per_range - 1)
+        for r in range(TOP):
             scaled = keep.tile([P, OWN], F32, name="scaled%d" % r)
-            for i in range(own_blocks):
+            for i, h in enumerate(halves):
                 c = r * blocks + i
-                nc.scalar.activation(
-                    scaled[:, i * P : (i + 1) * P], turned_own[:, i * P : (i + 1) * P], COPY, scale=gate_cols[:, c : c + 1]
-                )
-            for i in range(own_blocks):
-                first, last = r == 0 and i == 0, r == TOP - 1 and i == own_blocks - 1
-                turn(own_sum[:, i * P : (i + 1) * P], scaled[:, i * P : (i + 1) * P], first, last)
-        for j in range(ranges):
-            turned = keep.tile([P, RANGE], F32, name="turned%d" % j)
-            nc.scalar.copy(turned[:], sums[j][:, 0:RANGE])
-            for i in range(per_range):
-                turn(backs[j][:, i * P : (i + 1) * P], turned[:, i * P : (i + 1) * P], True, True)
-        own_res = keep.tile([P, OWN], F32, name="own_res")
-        nc.scalar.copy(own_res[:], own_sum[:, 0:OWN])
-        nc.sync.dma_start(out=out[:, 0:OWN], in_=own_res[:])
-        cut = STORES[-1][0]
-        fetch(TOP - 1, OWN, cut)
-        fetch(TOP - 1, cut, T)
-        for t0, t1 in STORES:
-            res = keep.tile([P, t1 - t0], F32, name="res%d" % t0)
-            o = t0 % RANGE
-            back = backs[(t0 - OWN) // RANGE]
-            nc.vector.tensor_tensor(res[:], back[:, o : o + t1 - t0], prods[TOP - 1][:, t0 - OWN : t1 - OWN], ADD)
-            nc.sync.dma_start(out=out[:, t0:t1], in_=res[:])
+                nc.scalar.activation(scaled[:, h], turned_own[r][:, h], COPY, scale=gate_cols[:, c : c + 1])
+            for i, h in enumerate(halves):
+                turn(own_sum[:, h], scaled[:, h], r == 0 and i == 0, r == TOP - 1 and i == per_range - 1)
+            if r == 1:
+                turned = keep.tile([P, RANGE], F32, name="turned")
+                nc.scalar.copy(turned[:], mid_sum[:, 0:RANGE])
+                for h in halves:
+                    turn(mid_back[:, h], turned[:, h], True, True)
+                store(OWN, mid_back)
+        store(0, own_sum)
+
+        t0 = OWN + RANGE
+        first, second, third = [fetch(r, t0, T) for r in range(TOP - 1)]
+        two = keep.tile([P, RANGE], F32, name="two")
+        nc.vector.tensor_tensor(two[:], first[:], second[:], ADD)
+        fourth = [fetch(TOP - 1, t0, t0 + P)]
+        three = keep.tile([P, RANGE], F32, name="three")
+        nc.vector.tensor_tensor(three[:], two[:], third[:], ADD)
+        fourth.append(fetch(TOP - 1, t0 + P, T))
+        for i, h in enumerate(halves):
+            res = keep.tile([P, P], F32, name="res%d" % (t0 + i * P))
+            nc.vector.tensor_tensor(res[:], three[:, h], fourth[i][:], ADD)
+            nc.sync.dma_start(out=out[:, t0 + i * P : t0 + (i + 1) * P], in_=res[:])

@@ -40,6 +40,7 @@ VECTOR_EXPERTS = 2
 W_LOAD = 8
 RANGE = 256
 OWN = 256
+LENT = 128
 
 
 def tile_moe_tk_lin_relu_kernel(
@@ -166,11 +167,13 @@ def tile_moe_tk_lin_relu_kernel(
         def turn(dst, src, start, stop):
             nc.tensor.matmul(out=dst, lhsT=src, rhs=ident[:], is_transpose=True, start=start, stop=stop)
 
+        def gates_of(r, t0, t1):
+            return gates[:, r * rest + t0 - OWN : r * rest + t1 - OWN]
+
         def fetch(r, t0, t1):
             prod = keep.tile([P, t1 - t0], F32, name="prod%d_%d" % (r, t0))
             entries = pos_ts[r][:, t0 // LANES : t1 // LANES]
-            gate_part = gates[:, r * rest + t0 - OWN : r * rest + t1 - OWN]
-            nc.vector.tensor_tensor(prod[:], y[:].indirect(entries), gate_part, MULT)
+            nc.vector.tensor_tensor(prod[:], y[:].indirect(entries), gates_of(r, t0, t1), MULT)
             return prod
 
         def store(t0, bank):
@@ -178,19 +181,30 @@ def tile_moe_tk_lin_relu_kernel(
             nc.scalar.copy(res[:], bank[:, 0:RANGE])
             nc.scalar.dma_start(out=out[:, t0 : t0 + RANGE], in_=res[:])
 
+        def add(name, a, c):
+            total = keep.tile([P, a.shape[1]], F32, name=name)
+            nc.vector.tensor_tensor(total[:], a, c, ADD)
+            return total
+
         per_range = RANGE // P
         halves = [slice(i * P, (i + 1) * P) for i in range(per_range)]
+        summed = T - RANGE
         mid_sum = psum.tile([P, BANK], F32, name="bank0")
         own_sum = psum.tile([P, BANK], F32, name="bank1")
         mid_back = psum.tile([P, BANK], F32, name="bank2")
         turned_own = []
         for r in range(TOP):
-            plain = keep.tile([P, OWN], F32, name="plain%d" % r)
-            nc.scalar.activation(plain[:], y[:].indirect(pos_ts[r][:, 0 : OWN // LANES]), COPY)
+            width = OWN + LENT if r == TOP - 1 else OWN
+            plain = keep.tile([P, width], F32, name="plain%d" % r)
+            nc.scalar.activation(plain[:], y[:].indirect(pos_ts[r][:, 0 : width // LANES]), COPY)
             turned_own.append(psum.tile([P, BANK], F32, name="bank%d" % (3 + r)))
             for h in halves:
                 turn(turned_own[r][:, h], plain[:, h], True, True)
-            prod = fetch(r, OWN, OWN + RANGE)
+            if r == 0:
+                first = fetch(r, OWN, T)
+                prod = first[:, RANGE:]
+            else:
+                prod = fetch(r, summed, T)
             for i, h in enumerate(halves):
                 turn(mid_sum[:, h], prod[:, h], r == 0 and i == 0, r == TOP - 1 and i == per_range - 1)
         for r in range(TOP):
@@ -200,23 +214,20 @@ def tile_moe_tk_lin_relu_kernel(
                 nc.scalar.activation(scaled[:, h], turned_own[r][:, h], COPY, scale=gate_cols[:, c : c + 1])
             for i, h in enumerate(halves):
                 turn(own_sum[:, h], scaled[:, h], r == 0 and i == 0, r == TOP - 1 and i == per_range - 1)
-            if r == 1:
-                turned = keep.tile([P, RANGE], F32, name="turned")
-                nc.scalar.copy(turned[:], mid_sum[:, 0:RANGE])
-                for h in halves:
-                    turn(mid_back[:, h], turned[:, h], True, True)
-                store(OWN, mid_back)
+        turned = keep.tile([P, RANGE], F32, name="turned")
+        nc.scalar.copy(turned[:], mid_sum[:, 0:RANGE])
+        for h in halves:
+            turn(mid_back[:, h], turned[:, h], True, True)
         store(0, own_sum)
+        store(summed, mid_back)
 
-        t0 = OWN + RANGE
-        first, second, third = [fetch(r, t0, T) for r in range(TOP - 1)]
-        two = keep.tile([P, RANGE], F32, name="two")
-        nc.vector.tensor_tensor(two[:], first[:], second[:], ADD)
-        fourth = [fetch(TOP - 1, t0, t0 + P)]
-        three = keep.tile([P, RANGE], F32, name="three")
-        nc.vector.tensor_tensor(three[:], two[:], third[:], ADD)
-        fourth.append(fetch(TOP - 1, t0 + P, T))
-        for i, h in enumerate(halves):
-            res = keep.tile([P, P], F32, name="res%d" % (t0 + i * P))
-            nc.vector.tensor_tensor(res[:], three[:, h], fourth[i][:], ADD)
-            nc.sync.dma_start(out=out[:, t0 + i * P : t0 + (i + 1) * P], in_=res[:])
+        cut = OWN + LENT
+        second, third = [fetch(r, OWN, summed) for r in (1, 2)]
+        two = add("two", first[:, 0:RANGE], second[:])
+        fourth = fetch(TOP - 1, cut, summed)
+        three = add("three", two[:], third[:])
+        lent = keep.tile([P, LENT], F32, name="lent")
+        nc.vector.tensor_tensor(lent[:], plain[:, OWN:], gates_of(TOP - 1, OWN, cut), MULT)
+        for t0, t1, last in ((cut, summed, fourth), (OWN, cut, lent)):
+            res = add("res%d" % t0, three[:, t0 - OWN : t1 - OWN], last[:])
+            nc.sync.dma_start(out=out[:, t0:t1], in_=res[:])

@@ -40,7 +40,7 @@ VECTOR_EXPERTS = 2
 W_LOAD = 8
 RANGE = 256
 OWN = 256
-LENT = 128
+STORES = ((256, 512), (512, 640), (640, 768))
 
 
 def tile_moe_tk_lin_relu_kernel(
@@ -167,67 +167,43 @@ def tile_moe_tk_lin_relu_kernel(
         def turn(dst, src, start, stop):
             nc.tensor.matmul(out=dst, lhsT=src, rhs=ident[:], is_transpose=True, start=start, stop=stop)
 
-        def gates_of(r, t0, t1):
-            return gates[:, r * rest + t0 - OWN : r * rest + t1 - OWN]
-
-        def fetch(r, t0, t1):
-            prod = keep.tile([P, t1 - t0], F32, name="prod%d_%d" % (r, t0))
-            entries = pos_ts[r][:, t0 // LANES : t1 // LANES]
-            nc.vector.tensor_tensor(prod[:], y[:].indirect(entries), gates_of(r, t0, t1), MULT)
+        def fetch(r):
+            prod = keep.tile([P, rest], F32, name="prod%d" % r)
+            entries = pos_ts[r][:, OWN // LANES :]
+            nc.vector.tensor_tensor(prod[:], y[:].indirect(entries), gates[:, r * rest : (r + 1) * rest], MULT)
             return prod
 
-        def store(t0, bank):
-            res = keep.tile([P, RANGE], F32, name="res%d" % t0)
-            nc.scalar.copy(res[:], bank[:, 0:RANGE])
-            nc.scalar.dma_start(out=out[:, t0 : t0 + RANGE], in_=res[:])
-
-        def add(name, a, c):
-            total = keep.tile([P, a.shape[1]], F32, name=name)
-            nc.vector.tensor_tensor(total[:], a, c, ADD)
-            return total
-
-        per_range = RANGE // P
-        halves = [slice(i * P, (i + 1) * P) for i in range(per_range)]
-        summed = T - RANGE
-        mid_sum = psum.tile([P, BANK], F32, name="bank0")
-        own_sum = psum.tile([P, BANK], F32, name="bank1")
-        mid_back = psum.tile([P, BANK], F32, name="bank2")
+        halves = [slice(i * P, (i + 1) * P) for i in range(OWN // P)]
+        own_sums = [psum.tile([P, BANK], F32, name="bank%d" % (TOP + 1 + i)) for i in range(len(halves))]
         turned_own = []
         for r in range(TOP):
-            width = OWN + LENT if r == TOP - 1 else OWN
+            width = T if r == TOP - 1 else OWN
             plain = keep.tile([P, width], F32, name="plain%d" % r)
             nc.scalar.activation(plain[:], y[:].indirect(pos_ts[r][:, 0 : width // LANES]), COPY)
-            turned_own.append(psum.tile([P, BANK], F32, name="bank%d" % (3 + r)))
+            turned_own.append(psum.tile([P, BANK], F32, name="bank%d" % (1 + r)))
             for h in halves:
                 turn(turned_own[r][:, h], plain[:, h], True, True)
-            if r == 0:
-                first = fetch(r, OWN, T)
-                prod = first[:, RANGE:]
-            else:
-                prod = fetch(r, summed, T)
-            for i, h in enumerate(halves):
-                turn(mid_sum[:, h], prod[:, h], r == 0 and i == 0, r == TOP - 1 and i == per_range - 1)
         for r in range(TOP):
             scaled = keep.tile([P, OWN], F32, name="scaled%d" % r)
             for i, h in enumerate(halves):
                 c = r * blocks + i
                 nc.scalar.activation(scaled[:, h], turned_own[r][:, h], COPY, scale=gate_cols[:, c : c + 1])
             for i, h in enumerate(halves):
-                turn(own_sum[:, h], scaled[:, h], r == 0 and i == 0, r == TOP - 1 and i == per_range - 1)
-        turned = keep.tile([P, RANGE], F32, name="turned")
-        nc.scalar.copy(turned[:], mid_sum[:, 0:RANGE])
-        for h in halves:
-            turn(mid_back[:, h], turned[:, h], True, True)
-        store(0, own_sum)
-        store(summed, mid_back)
+                turn(own_sums[i][:, 0:P], scaled[:, h], r == 0, r == TOP - 1)
+        own_res = keep.tile([P, OWN], F32, name="own_res")
+        for i, h in enumerate(halves):
+            nc.scalar.copy(own_res[:, h], own_sums[i][:, 0:P])
+        nc.sync.dma_start(out=out[:, 0:OWN], in_=own_res[:])
 
-        cut = OWN + LENT
-        second, third = [fetch(r, OWN, summed) for r in (1, 2)]
-        two = add("two", first[:, 0:RANGE], second[:])
-        fourth = fetch(TOP - 1, cut, summed)
-        three = add("three", two[:], third[:])
-        lent = keep.tile([P, LENT], F32, name="lent")
-        nc.vector.tensor_tensor(lent[:], plain[:, OWN:], gates_of(TOP - 1, OWN, cut), MULT)
-        for t0, t1, last in ((cut, summed, fourth), (OWN, cut, lent)):
-            res = add("res%d" % t0, three[:, t0 - OWN : t1 - OWN], last[:])
+        first, second, third = [fetch(r) for r in range(TOP - 1)]
+        two = keep.tile([P, rest], F32, name="two")
+        nc.vector.tensor_tensor(two[:], first[:], second[:], ADD)
+        fourth = keep.tile([P, rest], F32, name="fourth")
+        nc.vector.tensor_tensor(fourth[:], plain[:, OWN:], gates[:, (TOP - 1) * rest :], MULT)
+        three = keep.tile([P, rest], F32, name="three")
+        for t0 in range(0, rest, RANGE):
+            nc.vector.tensor_tensor(three[:, t0 : t0 + RANGE], two[:, t0 : t0 + RANGE], third[:, t0 : t0 + RANGE], ADD)
+        for t0, t1 in STORES:
+            res = keep.tile([P, t1 - t0], F32, name="res%d" % t0)
+            nc.vector.tensor_tensor(res[:], three[:, t0 - OWN : t1 - OWN], fourth[:, t0 - OWN : t1 - OWN], ADD)
             nc.sync.dma_start(out=out[:, t0:t1], in_=res[:])

@@ -39,8 +39,8 @@ VECTOR_EXPERTS = 2
 
 W_LOAD = 8
 RANGE = 256
-OWN = 256
-STORES = ((256, 512), (512, 640), (640, 768))
+OWN = (384, 384, 384, 256)
+CUT = 640
 
 
 def tile_moe_tk_lin_relu_kernel(
@@ -123,14 +123,15 @@ def tile_moe_tk_lin_relu_kernel(
         nc.tensor.transpose(turned_rows[:, 0:P], gate_rows[:], ident[:])
         gate_cols = keep.tile([P, TOP * blocks], F32, name="gate_cols")
         nc.scalar.copy(gate_cols[:], turned_rows[:, 0 : TOP * blocks])
-        rest = T - OWN
-        gates = keep.tile([P, TOP * rest], F32, name="gates")
+        gates = []
         for r in range(TOP):
             spread = psum.tile([P, BANK], F32, name="bank%d" % r)
-            for i in range(rest // P):
-                c = r * blocks + OWN // P + i
-                nc.tensor.transpose(spread[:, i * P : (i + 1) * P], gate_cols[:, c : c + 1].to_broadcast([P, P]), ident[:])
-            nc.scalar.copy(gates[:, r * rest : (r + 1) * rest], spread[:, 0:rest])
+            for i in range(OWN[r] // P, blocks):
+                c = r * blocks + i
+                o = i * P - OWN[r]
+                nc.tensor.transpose(spread[:, o : o + P], gate_cols[:, c : c + 1].to_broadcast([P, P]), ident[:])
+            gates.append(keep.tile([P, T - OWN[r]], F32, name="gates%d" % r))
+            nc.scalar.copy(gates[r][:], spread[:, 0 : T - OWN[r]])
 
         y = keep.tile([P, S], F32, name="y")
 
@@ -168,42 +169,43 @@ def tile_moe_tk_lin_relu_kernel(
             nc.tensor.matmul(out=dst, lhsT=src, rhs=ident[:], is_transpose=True, start=start, stop=stop)
 
         def fetch(r):
-            prod = keep.tile([P, rest], F32, name="prod%d" % r)
-            entries = pos_ts[r][:, OWN // LANES :]
-            nc.vector.tensor_tensor(prod[:], y[:].indirect(entries), gates[:, r * rest : (r + 1) * rest], MULT)
+            prod = keep.tile([P, T - OWN[r]], F32, name="prod%d" % r)
+            nc.vector.tensor_tensor(prod[:], y[:].indirect(pos_ts[r][:, OWN[r] // LANES :]), gates[r][:], MULT)
             return prod
 
-        halves = [slice(i * P, (i + 1) * P) for i in range(OWN // P)]
-        own_sums = [psum.tile([P, BANK], F32, name="bank%d" % (TOP + 1 + i)) for i in range(len(halves))]
-        turned_own = []
+        turned = []
         for r in range(TOP):
-            width = T if r == TOP - 1 else OWN
-            plain = keep.tile([P, width], F32, name="plain%d" % r)
-            nc.scalar.activation(plain[:], y[:].indirect(pos_ts[r][:, 0 : width // LANES]), COPY)
-            turned_own.append(psum.tile([P, BANK], F32, name="bank%d" % (1 + r)))
-            for h in halves:
-                turn(turned_own[r][:, h], plain[:, h], True, True)
+            plain = keep.tile([P, OWN[r]], F32, name="plain%d" % r)
+            nc.scalar.activation(plain[:], y[:].indirect(pos_ts[r][:, 0 : OWN[r] // LANES]), COPY)
+            turned.append(psum.tile([P, BANK], F32, name="bank%d" % (1 + r)))
+            for o in range(0, OWN[r], P):
+                turn(turned[r][:, o : o + P], plain[:, o : o + P], True, True)
+        own_blocks = max(OWN) // P
+        sums = [psum.tile([P, BANK], F32, name="bank%d" % (TOP + 1 + i)) for i in range(own_blocks)]
         for r in range(TOP):
-            scaled = keep.tile([P, OWN], F32, name="scaled%d" % r)
-            for i, h in enumerate(halves):
+            scaled = keep.tile([P, OWN[r]], F32, name="scaled%d" % r)
+            for i in reversed(range(OWN[r] // P)):
                 c = r * blocks + i
-                nc.scalar.activation(scaled[:, h], turned_own[r][:, h], COPY, scale=gate_cols[:, c : c + 1])
-            for i, h in enumerate(halves):
-                turn(own_sums[i][:, 0:P], scaled[:, h], r == 0, r == TOP - 1)
-        own_res = keep.tile([P, OWN], F32, name="own_res")
-        for i, h in enumerate(halves):
-            nc.scalar.copy(own_res[:, h], own_sums[i][:, 0:P])
-        nc.sync.dma_start(out=out[:, 0:OWN], in_=own_res[:])
+                h = slice(i * P, (i + 1) * P)
+                nc.scalar.activation(scaled[:, h], turned[r][:, h], COPY, scale=gate_cols[:, c : c + 1])
+                turn(sums[i][:, 0:P], scaled[:, h], r == 0, r == TOP - 1 or OWN[r + 1] <= i * P)
+        res = keep.tile([P, T], F32, name="res")
+        for i in reversed(range(OWN[-1] // P)):
+            nc.scalar.copy(res[:, i * P : (i + 1) * P], sums[i][:, 0:P])
 
+        shared = OWN[0] - OWN[-1]
         first, second, third = [fetch(r) for r in range(TOP - 1)]
-        two = keep.tile([P, rest], F32, name="two")
+        two = keep.tile([P, T - OWN[0]], F32, name="two")
         nc.vector.tensor_tensor(two[:], first[:], second[:], ADD)
-        fourth = keep.tile([P, rest], F32, name="fourth")
-        nc.vector.tensor_tensor(fourth[:], plain[:, OWN:], gates[:, (TOP - 1) * rest :], MULT)
-        three = keep.tile([P, rest], F32, name="three")
-        for t0 in range(0, rest, RANGE):
-            nc.vector.tensor_tensor(three[:, t0 : t0 + RANGE], two[:, t0 : t0 + RANGE], third[:, t0 : t0 + RANGE], ADD)
-        for t0, t1 in STORES:
-            res = keep.tile([P, t1 - t0], F32, name="res%d" % t0)
-            nc.vector.tensor_tensor(res[:], three[:, t0 - OWN : t1 - OWN], fourth[:, t0 - OWN : t1 - OWN], ADD)
-            nc.sync.dma_start(out=out[:, t0:t1], in_=res[:])
+        fourth = fetch(TOP - 1)
+        three = keep.tile([P, T - OWN[0]], F32, name="three")
+        parts = ((0, CUT - OWN[0]), (CUT - OWN[0], T - OWN[0]))
+        for c0, c1 in parts:
+            nc.vector.tensor_tensor(three[:, c0:c1], two[:, c0:c1], third[:, c0:c1], ADD)
+        for c0, c1 in parts:
+            t0, t1 = OWN[0] + c0, OWN[0] + c1
+            nc.vector.tensor_tensor(res[:, t0:t1], three[:, c0:c1], fourth[:, shared + c0 : shared + c1], ADD)
+            nc.sync.dma_start(out=out[:, t0:t1], in_=res[:, t0:t1])
+        nc.vector.tensor_tensor(res[:, OWN[-1] : OWN[0]], sums[-1][:, 0:shared], fourth[:, 0:shared], ADD)
+        nc.sync.dma_start(out=out[:, P : OWN[0]], in_=res[:, P : OWN[0]])
+        nc.sync.dma_start(out=out[:, 0:P], in_=res[:, 0:P])

@@ -40,7 +40,7 @@ VECTOR_EXPERTS = 2
 W_LOAD = 8
 RANGE = 256
 OWN = (384, 384, 384, 256)
-CUT = 640
+CUT = 512
 
 
 def tile_moe_tk_lin_relu_kernel(
@@ -199,13 +199,12 @@ def tile_moe_tk_lin_relu_kernel(
         nc.vector.tensor_tensor(two[:], first[:], second[:], ADD)
         fourth = fetch(TOP - 1)
         three = keep.tile([P, T - OWN[0]], F32, name="three")
-        parts = ((0, CUT - OWN[0]), (CUT - OWN[0], T - OWN[0]))
+        parts = ((CUT - OWN[0], T - OWN[0]), (0, CUT - OWN[0]))
         for c0, c1 in parts:
             nc.vector.tensor_tensor(three[:, c0:c1], two[:, c0:c1], third[:, c0:c1], ADD)
         for c0, c1 in parts:
             t0, t1 = OWN[0] + c0, OWN[0] + c1
             nc.vector.tensor_tensor(res[:, t0:t1], three[:, c0:c1], fourth[:, shared + c0 : shared + c1], ADD)
-            nc.sync.dma_start(out=out[:, t0:t1], in_=res[:, t0:t1])
         nc.vector.tensor_tensor(res[:, OWN[-1] : OWN[0]], sums[-1][:, 0:shared], fourth[:, 0:shared], ADD)
-        nc.sync.dma_start(out=out[:, P : OWN[0]], in_=res[:, P : OWN[0]])
-        nc.sync.dma_start(out=out[:, 0:P], in_=res[:, 0:P])
+        for t0, t1 in ((CUT, T), (OWN[-1], CUT), (P, OWN[-1]), (0, P)):
+            nc.sync.dma_start(out=out[:, t0:t1], in_=res[:, t0:t1])

@@ -57,7 +57,7 @@ def tile_moe_tk_lin_relu_kernel(
         nc.scalar.activation(warm_out[:], warm[:], RELU)
 
         x_bytes = keep.tile([P, WINDOW], U8, align_bytes=64, name="x_bytes")
-        nc.gpsimd.memset(x_bytes[:, 0:T], 0)
+        nc.vector.memset(x_bytes[:, 0:T].bitcast(I32), 0)
         w_bytes = keep.tile([P, E, N], U8, align_bytes=64, name="w_bytes")
         nc.vector.memset(w_bytes[:].rearrange("p e n -> p (e n)").bitcast(I32), 0)
 
@@ -65,7 +65,7 @@ def tile_moe_tk_lin_relu_kernel(
         make_identity(nc, ident[:])
         blocks = T // P
         gate_rows = keep.tile([P, P], F32, name="gate_rows")
-        nc.gpsimd.memset(gate_rows[:], 0.0)
+        nc.vector.memset(gate_rows[:], 0.0)
 
         x_view = xT.rearrange("(p j) w -> p j w", j=PACK)
         raws = []

@@ -182,13 +182,14 @@ def tile_moe_tk_lin_relu_kernel(
                 turn(turned[r][:, o : o + P], plain[:, o : o + P], True, True)
         own_blocks = max(OWN) // P
         sums = [psum.tile([P, BANK], F32, name="bank%d" % (TOP + 1 + i)) for i in range(own_blocks)]
-        for r in range(TOP):
-            scaled = keep.tile([P, OWN[r]], F32, name="scaled%d" % r)
-            for i in reversed(range(OWN[r] // P)):
-                c = r * blocks + i
-                h = slice(i * P, (i + 1) * P)
-                nc.scalar.activation(scaled[:, h], turned[r][:, h], COPY, scale=gate_cols[:, c : c + 1])
-                turn(sums[i][:, 0:P], scaled[:, h], r == 0, r == TOP - 1 or OWN[r + 1] <= i * P)
+        scaled = [keep.tile([P, OWN[r]], F32, name="scaled%d" % r) for r in range(TOP)]
+        order = [(0, i) for i in reversed(range(own_blocks))]
+        order = order + [(r, i) for i in reversed(range(own_blocks)) for r in range(1, TOP) if OWN[r] > i * P]
+        for r, i in order:
+            c = r * blocks + i
+            h = slice(i * P, (i + 1) * P)
+            nc.scalar.activation(scaled[r][:, h], turned[r][:, h], COPY, scale=gate_cols[:, c : c + 1])
+            turn(sums[i][:, 0:P], scaled[r][:, h], r == 0, r == TOP - 1 or OWN[r + 1] <= i * P)
         res = keep.tile([P, T], F32, name="res")
         for i in reversed(range(OWN[-1] // P)):
             nc.scalar.copy(res[:, i * P : (i + 1) * P], sums[i][:, 0:P])
@@ -206,5 +207,5 @@ def tile_moe_tk_lin_relu_kernel(
             t0, t1 = OWN[0] + c0, OWN[0] + c1
             nc.vector.tensor_tensor(res[:, t0:t1], three[:, c0:c1], fourth[:, shared + c0 : shared + c1], ADD)
         nc.vector.tensor_tensor(res[:, OWN[-1] : OWN[0]], sums[-1][:, 0:shared], fourth[:, 0:shared], ADD)
-        for t0, t1 in ((CUT, T), (OWN[-1], CUT), (P, OWN[-1]), (0, P)):
+        for t0, t1 in ((CUT, T), (P, OWN[-1]), (OWN[-1], CUT), (0, P)):
             nc.sync.dma_start(out=out[:, t0:t1], in_=res[:, t0:t1])

from contextlib import ExitStack

import concourse.mybir as mybir
from concourse.masks import make_identity

K, T, E, C, N, TOP = 512, 768, 24, 128, 128, 4
P = 128
PACK = 4
S = E * C
FLOPS = 2 * K * N * S

F32 = mybir.dt.float32
BF16 = mybir.dt.bfloat16
U32 = mybir.dt.uint32
I32 = mybir.dt.int32
U16 = mybir.dt.uint16
U8 = mybir.dt.uint8
FP8X4 = mybir.dt.float8_e4m3fn_x4
FP4X4 = mybir.dt.float4_e2m1fn_x4
ADD, MULT, MAX = mybir.AluOpType.add, mybir.AluOpType.mult, mybir.AluOpType.max
RELU = mybir.ActivationFunctionType.Relu
COPY = mybir.ActivationFunctionType.Copy

LANES = 16
BANKS = 8
BANK = 512

X_LOADS = ((256, 128), (256,), (128,))
VECTOR_EIGHTHS = 5

WINDOW = 4096
SHORT_WINDOW = 1024
SHORT_GATHER = 4

WORDS, SCALES = 0, 1
GATHERS = ((WORDS, 16), (SCALES, 16), (WORDS, 8), (SCALES, 4), (SCALES, 3), (SCALES, 1))
PACED_BANKS = 5
VECTOR_EXPERTS = 2

W_LOAD = 8
RANGE = 256
OWN = (384, 384, 384, 256)
CUT = 512


def tile_moe_tk_lin_relu_kernel(
    tc, xT, w_words, w_scales, b, gate, offs, pos1, pos2, pos3, pos4, out
):
    nc = tc.nc
    with ExitStack() as ctx:
        keep = ctx.enter_context(tc.tile_pool(name="keep", bufs=1))
        psum = ctx.enter_context(tc.psum_pool(name="psum", bufs=1))

        warm = keep.tile([P, 8], F32, name="warm")
        nc.vector.memset(warm[:], 0.0)
        warm_out = keep.tile([P, 8], F32, name="warm_out")
        nc.scalar.activation(warm_out[:], warm[:], RELU)

        x_bytes = keep.tile([P, WINDOW], U8, align_bytes=64, name="x_bytes")
        nc.vector.memset(x_bytes[:, 0:T].bitcast(I32), 0)
        w_bytes = keep.tile([P, E, N], U8, align_bytes=64, name="w_bytes")
        nc.vector.memset(w_bytes[:].rearrange("p e n -> p (e n)").bitcast(I32), 0)

        ident = keep.tile([P, P], F32, name="ident")
        make_identity(nc, ident[:])
        blocks = T // P
        gate_rows = keep.tile([P, P], F32, name="gate_rows")
        nc.vector.memset(gate_rows[:], 0.0)

        x_view = xT.rearrange("(p j) w -> p j w", j=PACK)
        raws = []
        t0 = 0
        for widths in X_LOADS:
            raw = keep.tile([P, PACK, sum(widths)], F32, name="raw%d" % t0)
            nc.sync.dma_start(out=raw[:], in_=x_view[:, :, t0 : t0 + sum(widths)])
            o = 0
            for width in widths:
                raws.append((raw[:, :, o : o + width], t0 + o, t0 + o + width))
                o = o + width
            t0 = t0 + o
        offs_t = keep.tile([P, S // LANES], U16, name="offs_t")
        nc.sync.dma_start(offs_t[:], offs)
        for r in range(TOP):
            nc.sync.dma_start(
                out=gate_rows[blocks * r : blocks * (r + 1), :], in_=gate[r, 0, :].rearrange("(k t) -> k t", t=P)
            )
        for q in range(4):
            nc.sync.dma_start(
                out=w_bytes[32 * q : 32 * q + 4, :, :].bitcast(I32),
                in_=w_scales[:, 0, 4 * q : 4 * q + 4, :].rearrange("e q n -> q e n").bitcast(I32),
            )
        bias = keep.tile([P, E], F32, name="bias")
        nc.sync.dma_start(out=bias[:], in_=b)
        ws = []
        for e0 in range(0, E, W_LOAD):
            w = keep.tile([P, W_LOAD, 2 * N], U8, align_bytes=64, name="w%d" % e0)
            nc.sync.dma_start(
                out=w[:].bitcast(I32),
                in_=w_words[e0 : e0 + W_LOAD, 0, :, :].rearrange("e p c -> p e c").bitcast(I32),
            )
            ws.append(w)
        pos_ts = []
        for r, pos in enumerate((pos1, pos2, pos3, pos4)):
            pos_t = keep.tile([P, T // LANES], U16, name="pos_t%d" % r)
            nc.sync.dma_start(pos_t[:], pos)
            pos_ts.append(pos_t)

        x_words = keep.tile([P, WINDOW], U32, align_bytes=64, name="x_words")
        for raw, t0, t1 in raws:
            share = (t1 - t0) * VECTOR_EIGHTHS // 8
            source = raw.rearrange("p j (c i) -> p c j i", i=2)
            grouped = keep.tile([P, t1 - t0, PACK], BF16, align_bytes=64, name="grouped%d" % t0)
            target = grouped[:].rearrange("p (c i) j -> p c j i", i=2)
            nc.scalar.copy(out=target[:, share // 2 :], in_=source[:, share // 2 :])
            nc.vector.tensor_copy(out=target[:, : share // 2], in_=source[:, : share // 2])
            nc.vector.quantize_mx(
                out=x_words[:, t0:t1].bitcast(FP8X4),
                scales=x_bytes[:, t0:t1],
                in_=grouped[:].rearrange("p w j -> p (w j)"),
            )

        turned_rows = psum.tile([P, BANK], F32, name="bank%d" % (BANKS - 1))
        nc.tensor.transpose(turned_rows[:, 0:P], gate_rows[:], ident[:])
        gate_cols = keep.tile([P, TOP * blocks], F32, name="gate_cols")
        nc.scalar.copy(gate_cols[:], turned_rows[:, 0 : TOP * blocks])
        gates = []
        for r in range(TOP):
            spread = psum.tile([P, BANK], F32, name="bank%d" % r)
            for i in range(OWN[r] // P, blocks):
                c = r * blocks + i
                o = i * P - OWN[r]
                nc.tensor.transpose(spread[:, o : o + P], gate_cols[:, c : c + 1].to_broadcast([P, P]), ident[:])
            gates.append(keep.tile([P, T - OWN[r]], F32, name="gates%d" % r))
            nc.scalar.copy(gates[r][:], spread[:, 0 : T - OWN[r]])

        y = keep.tile([P, S], F32, name="y")

        tables = (x_words, x_bytes)
        gathered = ([], [])
        done = 0
        paced = GATHERS[0][1]
        for sort, count in GATHERS:
            first = len(gathered[sort])
            picked = keep.tile([P, count * C], (U32, U8)[sort], align_bytes=64, name="picked%d_%d" % (sort, first))
            window = tables[sort][:, 0:SHORT_WINDOW] if count < SHORT_GATHER else tables[sort][:]
            entries = offs_t[:, first * C // LANES : (first + count) * C // LANES]
            nc.vector.tensor_copy(picked[:], window.indirect(entries))
            gathered[sort].extend([picked[:, i * C : (i + 1) * C] for i in range(count)])
            for e in range(done, min(len(gathered[WORDS]), len(gathered[SCALES]))):
                bank = e % PACED_BANKS if e < paced else (PACED_BANKS + e - paced) % BANKS
                acc = psum.tile([P, BANK], F32, name="bank%d" % bank)
                nc.tensor.matmul_mx(
                    out=acc[:, 0:C],
                    lhsT=ws[e // W_LOAD][:, e % W_LOAD, :].bitcast(FP4X4),
                    lhsT_scale=w_bytes[:, e, :],
                    rhs=gathered[WORDS][e].bitcast(FP8X4),
                    rhs_scale=gathered[SCALES][e],
                    start=True,
                    stop=True,
                )
                dst = y[:, e * C : (e + 1) * C]
                if E - 1 - VECTOR_EXPERTS <= e < E - 1:
                    nc.vector.tensor_scalar(dst, acc[:, 0:C], bias[:, e : e + 1], 0.0, op0=ADD, op1=MAX)
                else:
                    nc.scalar.activation(dst, acc[:, 0:C], RELU, bias=bias[:, e : e + 1])
                done = e + 1

        def turn(dst, src, start, stop):
            nc.tensor.matmul(out=dst, lhsT=src, rhs=ident[:], is_transpose=True, start=start, stop=stop)

        def fetch(r):
            prod = keep.tile([P, T - OWN[r]], F32, name="prod%d" % r)
            nc.vector.tensor_tensor(prod[:], y[:].indirect(pos_ts[r][:, OWN[r] // LANES :]), gates[r][:], MULT)
            return prod

        turned = []
        for r in range(TOP):
            plain = keep.tile([P, OWN[r]], F32, name="plain%d" % r)
            nc.scalar.activation(plain[:], y[:].indirect(pos_ts[r][:, 0 : OWN[r] // LANES]), COPY)
            turned.append(psum.tile([P, BANK], F32, name="bank%d" % (1 + r)))
            for o in range(0, OWN[r], P):
                turn(turned[r][:, o : o + P], plain[:, o : o + P], True, True)
        own_blocks = max(OWN) // P
        sums = [psum.tile([P, BANK], F32, name="bank%d" % (TOP + 1 + i)) for i in range(own_blocks)]
        scaled = [keep.tile([P, OWN[r]], F32, name="scaled%d" % r) for r in range(TOP)]
        order = [(0, i) for i in reversed(range(own_blocks))]
        order = order + [(r, i) for i in reversed(range(own_blocks)) for r in range(1, TOP) if OWN[r] > i * P]
        for r, i in order:
            c = r * blocks + i
            h = slice(i * P, (i + 1) * P)
            nc.scalar.activation(scaled[r][:, h], turned[r][:, h], COPY, scale=gate_cols[:, c : c + 1])
            turn(sums[i][:, 0:P], scaled[r][:, h], r == 0, r == TOP - 1 or OWN[r + 1] <= i * P)
        res = keep.tile([P, T], F32, name="res")
        for i in reversed(range(OWN[-1] // P)):
            nc.scalar.copy(res[:, i * P : (i + 1) * P], sums[i][:, 0:P])

        shared = OWN[0] - OWN[-1]
        first, second, third = [fetch(r) for r in range(TOP - 1)]
        two = keep.tile([P, T - OWN[0]], F32, name="two")
        nc.vector.tensor_tensor(two[:], first[:], second[:], ADD)
        fourth = fetch(TOP - 1)
        three = keep.tile([P, T - OWN[0]], F32, name="three")
        parts = ((CUT - OWN[0], T - OWN[0]), (0, CUT - OWN[0]))
        for c0, c1 in parts:
            nc.vector.tensor_tensor(three[:, c0:c1], two[:, c0:c1], third[:, c0:c1], ADD)
        for c0, c1 in parts:
            t0, t1 = OWN[0] + c0, OWN[0] + c1
            nc.vector.tensor_tensor(res[:, t0:t1], three[:, c0:c1], fourth[:, shared + c0 : shared + c1], ADD)
        nc.vector.tensor_tensor(res[:, OWN[-1] : OWN[0]], sums[-1][:, 0:shared], fourth[:, 0:shared], ADD)
        for t0, t1 in ((CUT, T), (P, OWN[-1]), (OWN[-1], CUT), (0, P)):
            nc.sync.dma_start(out=out[:, t0:t1], in_=res[:, t0:t1])
